import numpy as np, ml_dtypes
CORES = [24,25,26,27,28,29,30,31]
N = 8
BF = ml_dtypes.bfloat16
def gentries(a):
    return np.ascontiguousarray(a.reshape(8, 16, -1).transpose(0, 2, 1)).reshape(8, -1)
def gtable(e):
    e = np.asarray(e); return np.ascontiguousarray(e.reshape(8, -1, 16).transpose(0, 2, 1)).reshape(128, -1).astype(np.int32)
D, UG, B, A, NB, KG = 4, 8, 6, 2, 32, 16
U, V, E, S, K = 8 * UG, 2 ** B, 2 ** (A * B), 16 * NB, 8 * KG // N
def stored(c):
    return np.ascontiguousarray(c.reshape(N, 8, UG, NB, 16).transpose(0, 1, 4, 3, 2)).reshape(N, 128, -1).astype(np.int32)
def unstored(x):
    return np.ascontiguousarray(x.reshape(N, 8, 16, NB, UG).transpose(0, 1, 4, 3, 2)).reshape(N, U, S).astype(np.int64)
def pack(t, c, gv, wr):
    return {"tb": t.reshape(N, 8, -1).astype(np.float32).astype(BF), "x": stored(c), "give": np.stack([gtable(v.reshape(8, -1)) for v in gv]), "wires": np.stack([gtable(v.reshape(8, -1)) for v in wr])}
def draw(rng):
    return rng.integers(0, V, (N, 8, D, UG, E)), rng.integers(0, V, (N, U, S)), rng.integers(0, U, (N, 8, D, KG)), rng.integers(0, N * K, (N, 8, D, A, UG))
def setup_inputs(rng):
    return pack(*draw(rng))
def setup_inputs_ends(rng):
    t, c, gv, wr = draw(rng)
    t = rng.integers(0, 2, t.shape) * (V - 1); t[..., 0] = 0; t[..., E - 1] = V - 1; c = rng.integers(0, 2, c.shape) * (V - 1); c[:, :, 0] = 0; c[:, :, S - 1] = V - 1
    gv = rng.choice(np.array([0, UG - 1, UG, 7 * UG, U - 1]), gv.shape); wr = rng.choice(np.array([0, K - 1, K, N * K - K, N * K - 1]), wr.shape)
    return pack(t, c, gv, wr)
def setup_inputs_one(rng):
    t, c, gv, wr = draw(rng)
    gv[:] = gv[..., :1].copy(); wr[:] = wr[:, :, :, :1].copy(); q = rng.integers(0, N); wr[q] = wr[q][..., :1].copy()
    return pack(t, c, gv, wr)
def setup_inputs_next(rng):
    t, c, gv, wr = draw(rng)
    i = rng.integers(0, 2, (N, 8, D, UG, 1)) * (A - 1); t = (np.arange(E) >> (B * (A - 1 - i))) & (V - 1)
    wr = wr % K + K * ((np.arange(N) + 1) % N).reshape(N, 1, 1, 1, 1)
    return pack(t, c, gv, wr)
def setup_inputs_spread(rng):
    t, c, gv, wr = draw(rng)
    t = t >> rng.integers(0, B + 1, (N, 8, D, UG, 1)); c = c >> rng.integers(0, B + 1, (N, U, 1))
    gv = (rng.random(gv.shape) ** 3 * U).astype(np.int64); wr = (rng.random(wr.shape) ** 3 * (N * K)).astype(np.int64)
    return pack(t, c, gv, wr)
def check_inputs(d):
    bad = []
    for name, top in (("x", V), ("give", U), ("wires", N * K)):
        if not ((d[name] >= 0) & (d[name] < top)).all(): bad.append(name)
    t = d["tb"].astype(np.float32)
    if not ((t >= 0) & (t < V) & (np.floor(t) == t)).all(): bad.append("tb")
    return bad
def reference(tb, x, give, wires):
    t = tb.astype(np.float32).astype(np.int64).reshape(N, 8, D, UG, E)
    gv = np.stack([gentries(v) for v in give]).reshape(N, 8 * D * KG).reshape(N, 8, D, KG)
    wr = np.stack([gentries(v) for v in wires]).reshape(N, 8, D, A, UG)
    c = unstored(x)
    for l in range(D):
        lines = np.zeros((N, N * K, S), np.int64); new = np.zeros((N, U, S), np.int64)
        for q in range(N):
            lines[:, q * K:(q + 1) * K] = c[q][gv[q, :, l].reshape(-1)].reshape(N, K, S)
        for r in range(N):
            a = np.zeros((8, UG, S), np.int64)
            for i in range(A):
                a = a * V + lines[r][wr[r, :, l, i]]
            new[r] = np.take_along_axis(t[r, :, l], a, axis=2).reshape(U, S)
        c = new
    return {"y": np.asarray(stored(c), np.float32)}

@@ -1,0 +1,358 @@
+from concourse.bass import DstId, RemoteDMATransfer
+from concourse.mybir import dt, AluOpType, AxisListType, ActivationFunctionType
+
+BF, F32, I32, U16 = "bfloat16", "float32", "int32", "uint16"
+D = 4
+
+SCRATCH = {
+    "xi": ("sbuf", [128, 256], I32), "xb": ("sbuf", [128, 256], BF), "x0": ("sbuf", [128, 1024], BF),
+    "gi": ("sbuf", [128, 4], I32), "gf": ("sbuf", [128, 4], F32),
+    "wi": ("sbuf", [128, 4], I32), "wf": ("sbuf", [128, 4], F32),
+    "diag": ("sbuf", [128, 512], BF), "giveb": ("sbuf", [128, 512], BF),
+    "sel0": ("sbuf", [128, 256], BF), "sel1": ("sbuf", [128, 256], BF),
+    "offs": ("sbuf", [128, 256], U16), "rr": ("sbuf", [128, 4096], BF),
+    "tab0": ("sbuf", [128, 4096], BF), "tab1": ("sbuf", [128, 4096], BF), "tab3": ("sbuf", [128, 8192], BF),
+    "lst0": ("sbuf", [128, 64], U16), "lst1": ("sbuf", [128, 64], U16),
+    "ysb": ("sbuf", [128, 256], F32),
+    "pcol": ("sbuf", [128, 1], F32), "pint": ("sbuf", [128, 1], I32),
+    "rowe": ("sbuf", [128, 128], BF), "rowq": ("sbuf", [128, 128], BF), "rowa": ("sbuf", [128, 128], BF),
+    "row16": ("sbuf", [128, 16], BF), "rho3": ("sbuf", [128, 128], BF), "rho4": ("sbuf", [128, 128], BF),
+    "zrow": ("sbuf", [128, 144], BF),
+    "v0i": ("sbuf", [128, 8], I32), "v0j": ("sbuf", [128, 8], I32), "v0f": ("sbuf", [128, 8], F32),
+    "cvi": ("sbuf", [128, 8], I32), "cvj": ("sbuf", [128, 8], I32), "cvf": ("sbuf", [128, 8], F32),
+    "k4i": ("sbuf", [128, 4], I32), "k4j": ("sbuf", [128, 4], I32), "k4f": ("sbuf", [128, 4], F32),
+    "g16i": ("sbuf", [128, 1], I32), "g16f": ("sbuf", [128, 1], F32),
+    "p7i": ("sbuf", [128, 1], I32), "p7f": ("sbuf", [128, 1], F32),
+    "p3i": ("sbuf", [128, 1], I32), "p3f": ("sbuf", [128, 1], F32),
+    "hi": ("sbuf", [128, 1], I32), "hc": ("sbuf", [128, 4], F32),
+    "u2i": ("sbuf", [128, 1], I32), "u2f": ("sbuf", [128, 1], F32),
+    "ones": ("sbuf", [128, 128], BF), "amat": ("sbuf", [128, 128], BF), "bmat": ("sbuf", [128, 64], BF),
+    "base": ("sbuf", [128, 576], BF), "emat": ("sbuf", [128, 512], BF), "pmat": ("sbuf", [128, 768], BF),
+}
+for _e in range(4):
+    SCRATCH["gm%d" % _e] = ("sbuf", [128, 1024], BF)
+    SCRATCH["sb%d" % _e] = ("sbuf", [128, 512], BF)
+    SCRATCH["land%d" % _e] = ("sbuf", [128, 512], BF)
+    SCRATCH["psg%d" % _e] = ("psum", [128, 512], F32)
+for _n in ("psa0", "psa1", "psm", "psw"):
+    SCRATCH[_n] = ("psum", [128, 512], F32)
+
+SEMAPHORES = ["qv", "qs", "qp", "qg", "loc", "arr0", "arr1", "arr2", "arr3",
+              "dgive", "dwire", "dx", "dt0", "dt1", "dt2", "dt3", "dy"]
+
+
+def rank_program(g, core, T, topo):
+    rank = T.rank_of(core)
+    if rank is None:
+        return
+    cores = T.cores
+    N = len(cores)
+    Op = AluOpType
+    Copy = ActivationFunctionType.Copy
+    queues = {"v": g.vector, "s": g.scalar, "p": g.tensor, "g": g, "y": g.sync}
+    count = {}
+    seen = {}
+
+    def need(q, *tokens):
+        want = {}
+        for name, val in tokens:
+            want[name] = max(val, want.get(name, 0))
+        for name in sorted(want):
+            if seen.get((q, name), 0) < want[name]:
+                queues[q].wait_ge(T.sem[name], want[name])
+                seen[(q, name)] = want[name]
+
+    def done(q, inst):
+        name = "q" + q
+        count[name] = count.get(name, 0) + 1
+        inst.then_inc(T.sem[name], 1)
+        return (name, count[name])
+
+    def dma(q, out, in_, name):
+        count[name] = count.get(name, 0) + 16
+        queues[q].dma_start(out, in_).then_inc(T.sem[name], 16)
+        return (name, count[name])
+
+    def ts(out, in0, s1, s2, op0, op1=None):
+        if op1 is None:
+            return done("v", g.vector.tensor_scalar(out, in0, s1, s2, op0))
+        return done("v", g.vector.tensor_scalar(out, in0, s1, s2, op0, op1))
+
+    def vcopy(out, in_):
+        return done("v", g.vector.tensor_copy(out, in_))
+
+    def scopy(out, in_):
+        return done("s", g.scalar.activation(out, in_, Copy))
+
+    def iota(out, pattern, base, mult, small=True):
+        if not small:
+            return done("g", g.iota(out, pattern, base, mult))
+        return done("g", g.iota(out, pattern, base, mult, allow_small_or_imprecise_dtypes=True))
+
+    def mm(out, lhsT, rhs, start, stop):
+        return g.tensor.matmul(out, lhsT, rhs, start, stop)
+
+    t_give = dma("y", T.gi[:], T.give[:, :], "dgive")
+    t_x = dma("s", T.xi[:], T.x[:, :], "dx")
+    t_wire = dma("y", T.wi[:], T.wires[:, :], "dwire")
+    W = 8 * 4096
+    dma("y", T.tab0[0::2, :], T.tb[:, 0:W], "dt0")
+    t_tab = {0: dma("y", T.tab0[1::2, :], T.tb[:, 0:W], "dt0")}
+
+    i_pcol = iota(T.pcol[:], [[0, 1]], 0, 1)
+    i_pint = iota(T.pint[:], [[0, 1]], 0, 1, False)
+    i_rowe = iota(T.rowe[:], [[4, 4], [16, 32]], 0, 0)
+    i_rowq = iota(T.rowq[:], [[1, 128]], 0, 0)
+    i_v0 = iota(T.v0i[:], [[2, 8]], 0, 16, False)
+    i_cv = iota(T.cvi[:], [[-2, 8]], 0, 1, False)
+    i_rowa = iota(T.rowa[:], [[0, 16], [1, 8]], 0, 0)
+    i_row16 = iota(T.row16[:], [[1, 2], [2, 8]], 0, 0)
+    i_rho3 = iota(T.rho3[:], [[4, 2], [8, 16], [1, 4]], 0, 0)
+    i_rho4 = iota(T.rho4[:], [[1, 8], [8, 16]], 0, 0)
+    i_k4 = iota(T.k4i[:], [[-4, 4]], 0, 1, False)
+    i_z = iota(T.zrow[:], [[16, 9], [-1000, 16]], 15000, 0)
+
+    pc = T.pcol[:, 0:1]
+    c_ones = done("v", g.vector.memset(T.ones[:], 1.0))
+    need("v", i_pint)
+    a1 = ts(T.p7i[:], T.pint[:], 7, None, Op.bitwise_and)
+    a2 = ts(T.p3i[:], T.pint[:], 3, None, Op.arith_shift_right)
+    a3 = ts(T.hi[:], T.pint[:], 3, 1, Op.arith_shift_right, Op.bitwise_and)
+    need("v", i_rowe)
+    for s4 in range(4):
+        c_e = ts(T.emat[:, 128 * s4:128 * s4 + 128], T.rowe[:], float(s4), pc, Op.add, Op.is_equal)
+    need("v", a1, a2, a3)
+    c_p7 = vcopy(T.p7f[:], T.p7i[:])
+    c_p3 = vcopy(T.p3f[:], T.p3i[:])
+    for k, (m, a) in enumerate(((2.0, 0.0), (2.0, 1.0), (1.0, 0.0), (1.0, 2.0))):
+        c_hc = ts(T.hc[:, k:k + 1], T.hi[:], m, a, Op.mult, Op.add)
+    need("v", i_rowq, i_v0, i_cv)
+    b1 = ts(T.v0j[:], T.v0i[:], 511, None, Op.bitwise_and)
+    b2 = ts(T.cvj[:], T.cvi[:], 15, None, Op.bitwise_and)
+    ts(T.pmat[:, 0:128], T.rowq[:], pc, 64.0, Op.is_equal, Op.mult)
+    c_perm1 = ts(T.pmat[:, 128:256], T.rowq[:], pc, None, Op.is_equal)
+    need("v", b1, b2)
+    c_v0 = vcopy(T.v0f[:], T.v0j[:])
+    c_cv = ts(T.cvf[:], T.cvj[:], -1000.0, pc, Op.mult, Op.add)
+
+    need("v", t_give)
+    c_gf = ts(T.gf[:], T.gi[:], 2.0, None, Op.mult)
+    need("v", c_gf)
+    c_d0 = ts(T.diag[:, 0:128], T.rowq[:], pc, T.gf[:, 0:1], Op.is_equal, Op.mult)
+    need("p", c_ones, c_d0)
+    p_b0 = done("p", mm(T.psm[:, 0:128], T.ones[:], T.diag[:, 0:128], True, True))
+    need("v", t_x)
+    c_xb = vcopy(T.xb[:], T.xi[:])
+    need("s", p_b0)
+    s_b0 = scopy(T.giveb[:, 0:128], T.psm[:, 0:128])
+    need("p", c_xb, c_e)
+    p_x = [done("p", mm(T["psg%d" % s4][:, 0:256], T.emat[:, 128 * s4:128 * s4 + 128], T.xb[:], True, True)) for s4 in range(4)]
+    need("v", s_b0, c_v0)
+    for u in range(8):
+        c_g0 = ts(T.gm0[:, 128 * u:128 * u + 128], T.giveb[:, 0:128], T.v0f[:, u:u + 1], None, Op.is_equal)
+    for s4 in range(3):
+        need("s", p_x[s4])
+        s_x = scopy(T.x0[:, 256 * s4:256 * s4 + 256], T["psg%d" % s4][:, 0:256])
+    need("v", p_x[3])
+    c_x3 = vcopy(T.x0[:, 768:1024], T.psg3[:, 0:256])
+
+    def evac(q, e, c, tok):
+        need(q, tok)
+        out, in_ = T["sb%d" % e][:, c:512:4], T["psg%d" % c][:, 0:128]
+        return vcopy(out, in_) if q == "v" else scopy(out, in_)
+
+    others = [r for r in range(N) if r != rank]
+
+    def send(e, *tokens):
+        need("g", *tokens)
+        pools = [[], []]
+        for k, en in enumerate(topo.engines(core, cores[others[0]])):
+            pools[k % 2].append(en)
+        moves = []
+        for r in others:
+            dst = cores[r]
+            pool = pools[0 if topo.die(dst) != topo.die(core) else 1]
+            if len(pool) < 2:
+                pool = pools[0] if len(pools[0]) >= 2 else pools[1]
+            mask = 0
+            for _k in range(2):
+                mask |= 1 << pool.pop(0)
+            rid, pid = topo.addr(dst)[:2]
+            moves.append(RemoteDMATransfer(dst_ids=[DstId(rid=rid, pnc=pid)], dma_engine_mask=mask,
+                                           remote_sem=T.sem["arr%d" % e],
+                                           src=T["sb%d" % e][:, 64 * r:64 * r + 64],
+                                           dst=T["land%d" % e][:, 64 * rank:64 * rank + 64]))
+        g.remote_dma_fused(moves, local_sem=T.sem["loc"])
+        count["loc"] = count.get("loc", 0) + 2 * len(others)
+
+    def own(e, *tokens):
+        need("v", *tokens)
+        return vcopy(T["land%d" % e][:, 64 * rank:64 * rank + 64], T["sb%d" % e][:, 64 * rank:64 * rank + 64])
+
+    need("p", c_g0, c_x3, s_x)
+    p_g = []
+    for c in range(4):
+        for u in range(8):
+            inst = mm(T["psg%d" % c][:, 0:128], T.x0[32 * c:32 * c + 8, u:1024:8],
+                      T.gm0[32 * c:32 * c + 8, 128 * u:128 * u + 128], u == 0, u == 7)
+        p_g.append(done("p", inst))
+    for e in range(1, 4):
+        c_d = ts(T.diag[:, 128 * e:128 * e + 128], T.rowq[:], pc, T.gf[:, e:e + 1], Op.is_equal, Op.mult)
+    need("v", t_wire)
+    c_wf = vcopy(T.wf[:], T.wi[:])
+    need("v", i_rowa, i_row16, c_p7, c_p3, c_wf)
+    c_am = ts(T.amat[:], T.rowa[:], T.p7f[:, 0:1], None, Op.is_equal)
+    for l in range(4):
+        c_bm = ts(T.bmat[:, 16 * l:16 * l + 16], T.row16[:], T.p3f[:, 0:1], T.wf[:, l:l + 1], Op.is_equal, Op.mult)
+    ev = [evac("v", 0, 0, p_g[0]), evac("s", 0, 1, p_g[1]), evac("v", 0, 2, p_g[2]), evac("s", 0, 3, p_g[3])]
+    send(0, *ev)
+    t_own = own(0, *ev)
+
+    need("p", c_am, c_bm, c_d)
+    p_w = done("p", mm(T.psw[:, 0:64], T.amat[:], T.bmat[:], True, True))
+    p_b = done("p", mm(T.psm[:, 128:512], T.ones[:], T.diag[:, 128:512], True, True))
+    need("s", p_b)
+    s_b = scopy(T.giveb[:, 128:512], T.psm[:, 128:512])
+    need("v", p_w, c_hc)
+    for c2 in range(2):
+        lst = T["lst%d" % c2]
+        ts(lst[:, 0:48], T.psw[:, 0:48], 4.0, T.hc[:, c2:c2 + 1], Op.mult, Op.add)
+        c_l = ts(lst[:, 48:64], T.psw[:, 48:64], 4.0, T.hc[:, 2 + c2:3 + c2], Op.mult, Op.add)
+    gm = {}
+
+    def build_g(e):
+        need("v", s_b, c_cv)
+        for u in range(8):
+            gm[e] = ts(T["gm%d" % e][:, 128 * u:128 * u + 128], T.giveb[:, 128 * e:128 * e + 128], T.cvf[:, u:u + 1], None, Op.is_equal)
+
+    zero = []
+
+    def clear(k):
+        zero.append(done("v", g.vector.memset(T.tab3[:, 2048 * k:2048 * k + 2048], 0.0)))
+
+    build_g(1)
+    clear(0)
+
+    perms = {0: c_perm1, 1: c_perm1}
+    sig = [2 * (k & 7) + (k >> 3) for k in range(16)]
+    looks = []
+
+    for e in range(D):
+        last = e == D - 1
+        arr = ("arr%d" % e, 2 * len(others))
+        land, tab = T["land%d" % e], T["tab%d" % (0, 1, 0, 3)[e]]
+        need("v", arr, t_own, c_l)
+        v_sel = vcopy(T.sel0[:], land[:, 0:512].indirect(T.lst0[:, 16 * e:16 * e + 16]))
+        need("s", arr, t_own, c_l)
+        s_sel = scopy(T.sel1[:], land[:, 0:512].indirect(T.lst1[:, 16 * e:16 * e + 16]))
+        if not last:
+            need("y", arr)
+            lo = (e + 1) * W
+            if e == 0:
+                dma("y", T.tab1[0::2, :], T.tb[:, lo:lo + W], "dt1")
+                t_tab[1] = dma("y", T.tab1[1::2, :], T.tb[:, lo:lo + W], "dt1")
+            elif e == 1:
+                need("y", *looks)
+                t_tab[2] = dma("y", T.tab0[0::2, :], T.tb[:, lo:lo + W], "dt2")
+            else:
+                need("y", *zero)
+                dma("y", T.tab3[0::4, 0:4096], T.tb[:, lo:lo + W // 2], "dt3")
+                t_tab[3] = dma("y", T.tab3[2::4, 4096:8192], T.tb[:, lo + W // 2:lo + W], "dt3")
+        pk = (0, 0, 256, 512)[e]
+        pa = []
+        need("p", perms[e])
+        for c2, tok in ((0, v_sel), (1, s_sel)):
+            need("p", tok)
+            sel, ps = T["sel%d" % c2], T["psa%d" % c2]
+            mm(ps[:, 0:128], sel[:, 0:128], T.pmat[:, pk:pk + 128], True, False)
+            pa.append(done("p", mm(ps[:, 0:128], sel[:, 128:256], T.pmat[:, pk + 128:pk + 256], False, True)))
+        off = []
+
+        def address(c2):
+            need("v", pa[c2])
+            o, i = T.offs[:, 128 * c2:128 * c2 + 128], T["psa%d" % c2][:, 0:128]
+            off.append(ts(o, i, T.u2f[:, 0:1], None, Op.add) if last else vcopy(o, i))
+
+        def look(q, a, b):
+            need(q, t_tab[e], off[0 if b <= 128 else 1])
+            win = tab[:, 0:8192 if last else 4096].indirect(T.offs[:, a:b])
+            out = T.rr[:, 16 * a:16 * b]
+            return vcopy(out, win) if q == "v" else scopy(out, win)
+
+        if last:
+            need("v", c_u2)
+            pieces, at = [], 0
+            for n in (2, 2, 2, 1, 1):
+                pieces.append((at, at + n, at + 2 * n))
+                at += 2 * n
+            cut = [(16 * a, 16 * b, 16 * c) for a, b, c in pieces]
+        else:
+            cut = [(64 * j, 64 * j + 30, 64 * j + 64) for j in range(4)]
+        address(0)
+        vt, st = [], []
+        for j, (a, b, c) in enumerate(cut):
+            if j == 1:
+                address(1)
+            vt.append(look("v", a, b))
+        for j, (a, b, c) in enumerate(cut):
+            st.append(look("s", b, c))
+        looks = [vt[-1], st[-1]]
+        if not last:
+            p_g = []
+            for j in range(4):
+                need("p", vt[j], st[j], gm[e + 1])
+                for u in range(8):
+                    inst = mm(T["psg%d" % j][:, 0:128], T.rr[:, 1024 * j + u:1024 * j + 1024:8],
+                              T["gm%d" % (e + 1)][:, 128 * u:128 * u + 128], u == 0, u == 7)
+                p_g.append(done("p", inst))
+            ev = [evac("v", e + 1, 0, p_g[0]), evac("v", e + 1, 1, p_g[1]), evac("s", e + 1, 2, p_g[2]), evac("s", e + 1, 3, p_g[3])]
+            send(e + 1, *ev)
+            t_own = own(e + 1, *ev)
+            if e == 0:
+                build_g(2)
+                clear(1)
+                clear(2)
+            elif e == 1:
+                build_g(3)
+                need("v", i_rho3, i_rho4)
+                for k, rho in ((256, T.rho3), (512, T.rho4)):
+                    ts(T.pmat[:, k:k + 128], rho[:], pc, 64.0, Op.is_equal, Op.mult)
+                    c_p = ts(T.pmat[:, k + 128:k + 256], rho[:], pc, None, Op.is_equal)
+                perms[2] = perms[3] = c_p
+                clear(3)
+            else:
+                need("v", i_k4, i_z)
+                x1 = ts(T.k4j[:], T.k4i[:], 13, None, Op.bitwise_and)
+                x2 = ts(T.g16i[:], T.pint[:], 112, None, Op.bitwise_and)
+                x3 = ts(T.u2i[:], T.pint[:], 2, 1, Op.arith_shift_right, Op.bitwise_and)
+                need("v", x1, x2, x3)
+                x4 = vcopy(T.g16f[:], T.g16i[:])
+                c_u2 = ts(T.u2f[:], T.u2i[:], 4096.0, None, Op.mult)
+                need("v", x4)
+                x5 = ts(T.k4f[:], T.k4j[:], -1000.0, T.g16f[:, 0:1], Op.mult, Op.add)
+                need("v", x5)
+                for v in range(4):
+                    c_base = ts(T.base[:, 144 * v:144 * v + 144], T.zrow[:], T.k4f[:, v:v + 1], None, Op.is_equal)
+        else:
+            need("p", c_base)
+            blocks = []
+            for j, (a, b, c) in enumerate(pieces):
+                blocks += [(k, vt[j]) for k in range(a, b)] + [(k, st[j]) for k in range(b, c)]
+            p_y = {}
+            for n, (k, tok) in enumerate(blocks):
+                need("p", tok)
+                z = 15 - sig[k]
+                for v in range(4):
+                    inst = mm(T["psg%d" % v][:, 0:64], T.base[:, 144 * v + z:144 * v + z + 128],
+                              T.rr[:, 256 * k + v:256 * k + 256:4], n == 0, n == len(blocks) - 1)
+                    if n == len(blocks) - 1:
+                        p_y[v] = done("p", inst)
+            fin = []
+            for v, q in ((0, "v"), (1, "s"), (2, "v"), (3, "s")):
+                need(q, p_y[v])
+                out, in_ = T.ysb[:, v:256:4], T["psg%d" % v][:, 0:64]
+                fin.append(vcopy(out, in_) if q == "v" else scopy(out, in_))
+            need("y", *fin)
+            t_y = dma("y", T.y[:, :], T.ysb[:], "dy")
+            need("y", t_y)
+    need("g", *[(n, count[n]) for n in ("qv", "qs", "qp", "qg", "loc")])

@@ -4,41 +4,22 @@ from concourse.mybir import dt, AluOpType, AxisListType, ActivationFunctionType
 BF, F32, I32, U16 = "bfloat16", "float32", "int32", "uint16"
 D = 4
 
-SCRATCH = {
-    "xi": ("sbuf", [128, 256], I32), "xb": ("sbuf", [128, 256], BF), "x0": ("sbuf", [128, 1024], BF),
-    "gi": ("sbuf", [128, 4], I32), "gf": ("sbuf", [128, 4], F32),
-    "wi": ("sbuf", [128, 4], I32), "wf": ("sbuf", [128, 4], F32),
-    "diag": ("sbuf", [128, 512], BF), "giveb": ("sbuf", [128, 512], BF),
-    "sel0": ("sbuf", [128, 256], BF), "sel1": ("sbuf", [128, 256], BF),
-    "offs": ("sbuf", [128, 256], U16), "rr": ("sbuf", [128, 4096], BF),
-    "tab0": ("sbuf", [128, 4096], BF), "tab1": ("sbuf", [128, 4096], BF), "tab3": ("sbuf", [128, 8192], BF),
-    "lst0": ("sbuf", [128, 64], U16), "lst1": ("sbuf", [128, 64], U16),
-    "ysb": ("sbuf", [128, 256], F32),
-    "pcol": ("sbuf", [128, 1], F32), "pint": ("sbuf", [128, 1], I32),
-    "rowe": ("sbuf", [128, 128], BF), "rowq": ("sbuf", [128, 128], BF), "rowa": ("sbuf", [128, 128], BF),
-    "row16": ("sbuf", [128, 16], BF), "rho3": ("sbuf", [128, 128], BF), "rho4": ("sbuf", [128, 128], BF),
-    "zrow": ("sbuf", [128, 144], BF),
-    "v0i": ("sbuf", [128, 8], I32), "v0j": ("sbuf", [128, 8], I32), "v0f": ("sbuf", [128, 8], F32),
-    "cvi": ("sbuf", [128, 8], I32), "cvj": ("sbuf", [128, 8], I32), "cvf": ("sbuf", [128, 8], F32),
-    "k4i": ("sbuf", [128, 4], I32), "k4j": ("sbuf", [128, 4], I32), "k4f": ("sbuf", [128, 4], F32),
-    "g16i": ("sbuf", [128, 1], I32), "g16f": ("sbuf", [128, 1], F32),
-    "p7i": ("sbuf", [128, 1], I32), "p7f": ("sbuf", [128, 1], F32),
-    "p3i": ("sbuf", [128, 1], I32), "p3f": ("sbuf", [128, 1], F32),
-    "hi": ("sbuf", [128, 1], I32), "hc": ("sbuf", [128, 4], F32),
-    "u2i": ("sbuf", [128, 1], I32), "u2f": ("sbuf", [128, 1], F32),
-    "ones": ("sbuf", [128, 128], BF), "amat": ("sbuf", [128, 128], BF), "bmat": ("sbuf", [128, 64], BF),
-    "base": ("sbuf", [128, 576], BF), "emat": ("sbuf", [128, 512], BF), "pmat": ("sbuf", [128, 768], BF),
-}
-for _e in range(4):
-    SCRATCH["gm%d" % _e] = ("sbuf", [128, 1024], BF)
-    SCRATCH["sb%d" % _e] = ("sbuf", [128, 512], BF)
-    SCRATCH["land%d" % _e] = ("sbuf", [128, 512], BF)
-    SCRATCH["psg%d" % _e] = ("psum", [128, 512], F32)
-for _n in ("psa0", "psa1", "psm", "psw"):
+SCRATCH = {}
+for _t, _names in ((BF, "xb 256 xt 256 xr 256 diag 512 giveb 512 sel0 256 sel1 256 rr 4096 tab0 4096 tab1 4096 tab3 8192 rowq 128 "
+                        "rowa 128 row16 16 rho3 128 rho4 128 zrow 144 ones 128 amat 128 bmat 64 base 576 pmat 768 "
+                        "gm0 1024 gm1 1024 gm2 1024 gm3 1024 sb0 512 sb1 512 sb2 512 sb3 512 land0 512 land1 512 land2 512 land3 512"),
+                   (F32, "gf 4 wf 4 ysb 256 pcol 1 v0f 4 cvf 16 k4f 4 hc 4 kap 1 g16f 1 p7f 1 p3f 1 hf 1 u2f 1 p96f 1 taf 1 tauf 1"),
+                   (I32, "xi 256 gi 4 wi 4 pint 1 v0i 4 v0j 4 cvi 16 cvj 16 k4i 4 k4j 4 xli 16 g16i 1 p7i 1 p3i 1 hi 1 u2i 1 "
+                         "p96i 1 tai 1 taui 1"),
+                   (U16, "offs 256 lst0 64 lst1 64 xl 16")):
+    _w = _names.split()
+    for _k in range(0, len(_w), 2):
+        SCRATCH[_w[_k]] = ("sbuf", [128, int(_w[_k + 1])], _t)
+for _n in ("psg0", "psg1", "psg2", "psg3", "psa0", "psa1", "psm", "psw"):
     SCRATCH[_n] = ("psum", [128, 512], F32)
 
 SEMAPHORES = ["qv", "qs", "qp", "qg", "loc", "arr0", "arr1", "arr2", "arr3",
-              "dgive", "dwire", "dx", "dt0", "dt1", "dt2", "dt3", "dy"]
+              "dgive", "dwire", "dx", "dt0", "dt1", "dt3", "dy"]
 
 
 def rank_program(g, core, T, topo):
@@ -78,14 +59,13 @@ def rank_program(g, core, T, topo):
             return done("v", g.vector.tensor_scalar(out, in0, s1, s2, op0))
         return done("v", g.vector.tensor_scalar(out, in0, s1, s2, op0, op1))
 
-    def vcopy(out, in_):
-        return done("v", g.vector.tensor_copy(out, in_))
-
-    def scopy(out, in_):
+    def copy(q, out, in_):
+        if q == "v":
+            return done("v", g.vector.tensor_copy(out, in_))
         return done("s", g.scalar.activation(out, in_, Copy))
 
-    def iota(out, pattern, base, mult, small=True):
-        if not small:
+    def iota(out, pattern, base, mult, whole=False):
+        if whole:
             return done("g", g.iota(out, pattern, base, mult))
         return done("g", g.iota(out, pattern, base, mult, allow_small_or_imprecise_dtypes=True))
 
@@ -97,43 +77,50 @@ def rank_program(g, core, T, topo):
     t_wire = dma("y", T.wi[:], T.wires[:, :], "dwire")
     W = 8 * 4096
     dma("y", T.tab0[0::2, :], T.tb[:, 0:W], "dt0")
-    t_tab = {0: dma("y", T.tab0[1::2, :], T.tb[:, 0:W], "dt0")}
+    t_tab = {}
+    t_tab[0] = t_tab[1] = dma("y", T.tab0[1::2, :], T.tb[:, W:2 * W], "dt0")
 
+    i_pint = iota(T.pint[:], [[0, 1]], 0, 1, True)
     i_pcol = iota(T.pcol[:], [[0, 1]], 0, 1)
-    i_pint = iota(T.pint[:], [[0, 1]], 0, 1, False)
-    i_rowe = iota(T.rowe[:], [[4, 4], [16, 32]], 0, 0)
+    i_xl = iota(T.xli[:], [[16, 2], [32, 2], [4, 4]], 0, 0, True)
+    i_v0 = iota(T.v0i[:], [[-8, 4]], 0, 1, True)
     i_rowq = iota(T.rowq[:], [[1, 128]], 0, 0)
-    i_v0 = iota(T.v0i[:], [[2, 8]], 0, 16, False)
-    i_cv = iota(T.cvi[:], [[-2, 8]], 0, 1, False)
+    i_cv = iota(T.cvi[:], [[-1, 2], [-2, 8]], 0, 1, True)
     i_rowa = iota(T.rowa[:], [[0, 16], [1, 8]], 0, 0)
     i_row16 = iota(T.row16[:], [[1, 2], [2, 8]], 0, 0)
-    i_rho3 = iota(T.rho3[:], [[4, 2], [8, 16], [1, 4]], 0, 0)
-    i_rho4 = iota(T.rho4[:], [[1, 8], [8, 16]], 0, 0)
-    i_k4 = iota(T.k4i[:], [[-4, 4]], 0, 1, False)
+    i_rho3 = iota(T.rho3[:], [[1, 2], [2, 64]], 0, 0)
+    i_rho4 = iota(T.rho4[:], [[4, 32], [1, 2], [2, 2]], 0, 0)
+    i_k4 = iota(T.k4i[:], [[-4, 4]], 0, 1, True)
     i_z = iota(T.zrow[:], [[16, 9], [-1000, 16]], 15000, 0)
+    zero = []
+
+    def clear(q, k):
+        part = T.tab3[:, 2048 * k:2048 * k + 2048]
+        zero.append(iota(part, [[0, 2048]], 0, 0) if q == "g" else done("v", g.vector.memset(part, 0.0)))
 
     pc = T.pcol[:, 0:1]
     c_ones = done("v", g.vector.memset(T.ones[:], 1.0))
     need("v", i_pint)
-    a1 = ts(T.p7i[:], T.pint[:], 7, None, Op.bitwise_and)
-    a2 = ts(T.p3i[:], T.pint[:], 3, None, Op.arith_shift_right)
-    a3 = ts(T.hi[:], T.pint[:], 3, 1, Op.arith_shift_right, Op.bitwise_and)
-    need("v", i_rowe)
-    for s4 in range(4):
-        c_e = ts(T.emat[:, 128 * s4:128 * s4 + 128], T.rowe[:], float(s4), pc, Op.add, Op.is_equal)
-    need("v", a1, a2, a3)
-    c_p7 = vcopy(T.p7f[:], T.p7i[:])
-    c_p3 = vcopy(T.p3f[:], T.p3i[:])
-    for k, (m, a) in enumerate(((2.0, 0.0), (2.0, 1.0), (1.0, 0.0), (1.0, 2.0))):
-        c_hc = ts(T.hc[:, k:k + 1], T.hi[:], m, a, Op.mult, Op.add)
-    need("v", i_rowq, i_v0, i_cv)
-    b1 = ts(T.v0j[:], T.v0i[:], 511, None, Op.bitwise_and)
-    b2 = ts(T.cvj[:], T.cvi[:], 15, None, Op.bitwise_and)
-    ts(T.pmat[:, 0:128], T.rowq[:], pc, 64.0, Op.is_equal, Op.mult)
-    c_perm1 = ts(T.pmat[:, 128:256], T.rowq[:], pc, None, Op.is_equal)
-    need("v", b1, b2)
-    c_v0 = vcopy(T.v0f[:], T.v0j[:])
-    c_cv = ts(T.cvf[:], T.cvj[:], -1000.0, pc, Op.mult, Op.add)
+
+    def bits(name, shift, mask):
+        if shift:
+            return ts(T[name + "i"][:], T.pint[:], shift, mask, Op.arith_shift_right, Op.bitwise_and)
+        return ts(T[name + "i"][:], T.pint[:], mask, None, Op.bitwise_and)
+
+    for n, sh, mk in (("ta", 2, 3), ("tau", 0, 3), ("p7", 0, 7), ("p96", 0, 96), ("p3", 3, 15), ("h", 3, 1)):
+        x1 = bits(n, sh, mk)
+    need("v", x1)
+    for n in ("ta", "p7", "p96", "p3"):
+        copy("v", T[n + "f"][:], T[n + "i"][:])
+    need("v", i_v0, i_xl)
+    x2 = ts(T.v0j[:], T.v0i[:], 24, None, Op.bitwise_and)
+    need("v", x2)
+    ts(T.tauf[:], T.taui[:], 64.0, T.taf[:, 0:1], Op.mult, Op.add)
+    x3 = ts(T.kap[:], T.p7f[:], 2.0, T.p96f[:, 0:1], Op.mult, Op.add)
+    need("v", x3)
+    c_xl = ts(T.xl[:], T.xli[:], T.tauf[:, 0:1], None, Op.add)
+    c_v0 = ts(T.v0f[:], T.v0j[:], -1000.0, T.kap[:, 0:1], Op.mult, Op.add)
+    need("v", i_rowq)
 
     need("v", t_give)
     c_gf = ts(T.gf[:], T.gi[:], 2.0, None, Op.mult)
@@ -142,24 +129,25 @@ def rank_program(g, core, T, topo):
     need("p", c_ones, c_d0)
     p_b0 = done("p", mm(T.psm[:, 0:128], T.ones[:], T.diag[:, 0:128], True, True))
     need("v", t_x)
-    c_xb = vcopy(T.xb[:], T.xi[:])
+    c_xb = copy("v", T.xb[:], T.xi[:])
+    need("v", c_xb)
+    c_xt = done("v", g.vector.transpose(T.xt[:], T.xb[:]))
     need("s", p_b0)
-    s_b0 = scopy(T.giveb[:, 0:128], T.psm[:, 0:128])
-    need("p", c_xb, c_e)
-    p_x = [done("p", mm(T["psg%d" % s4][:, 0:256], T.emat[:, 128 * s4:128 * s4 + 128], T.xb[:], True, True)) for s4 in range(4)]
+    s_b0 = copy("s", T.giveb[:, 0:128], T.psm[:, 0:128])
+    xr = []
+    for q, k in (("s", 1), ("v", 0)):
+        need(q, c_xt, c_xl)
+        xr.append(copy(q, T.xr[:, 128 * k:128 * k + 128], T.xt[:, 0:256].indirect(T.xl[:, 8 * k:8 * k + 8])))
     need("v", s_b0, c_v0)
-    for u in range(8):
-        c_g0 = ts(T.gm0[:, 128 * u:128 * u + 128], T.giveb[:, 0:128], T.v0f[:, u:u + 1], None, Op.is_equal)
-    for s4 in range(3):
-        need("s", p_x[s4])
-        s_x = scopy(T.x0[:, 256 * s4:256 * s4 + 256], T["psg%d" % s4][:, 0:256])
-    need("v", p_x[3])
-    c_x3 = vcopy(T.x0[:, 768:1024], T.psg3[:, 0:256])
-
-    def evac(q, e, c, tok):
-        need(q, tok)
-        out, in_ = T["sb%d" % e][:, c:512:4], T["psg%d" % c][:, 0:128]
-        return vcopy(out, in_) if q == "v" else scopy(out, in_)
+    need("p", *xr)
+    p_g = []
+    for c in range(4):
+        for g2 in range(2):
+            k = 2 * c + g2
+            tok = ts(T.gm0[:, 128 * k:128 * k + 128], T.giveb[:, 0:128], -16.0 * g2, T.v0f[:, c:c + 1], Op.add, Op.is_equal)
+            need("p", tok)
+            inst = mm(T["psg%d" % c][:, 0:128], T.xr[:, 128 * g2:128 * g2 + 128], T.gm0[:, 128 * k:128 * k + 128], g2 == 0, g2 == 1)
+        p_g.append(done("p", inst))
 
     others = [r for r in range(N) if r != rank]
 
@@ -185,35 +173,39 @@ def rank_program(g, core, T, topo):
         g.remote_dma_fused(moves, local_sem=T.sem["loc"])
         count["loc"] = count.get("loc", 0) + 2 * len(others)
 
-    def own(e, *tokens):
-        need("v", *tokens)
-        return vcopy(T["land%d" % e][:, 64 * rank:64 * rank + 64], T["sb%d" % e][:, 64 * rank:64 * rank + 64])
+    def handover(e, p_g):
+        ev = []
+        for c, q in enumerate("vvss" if e else "vsvs"):
+            need(q, p_g[c])
+            ev.append(copy(q, T["sb%d" % e][:, c:512:4], T["psg%d" % c][:, 0:128]))
+        send(e, *ev)
+        need("v", *ev)
+        return copy("v", T["land%d" % e][:, 64 * rank:64 * rank + 64], T["sb%d" % e][:, 64 * rank:64 * rank + 64])
 
-    need("p", c_g0, c_x3, s_x)
-    p_g = []
-    for c in range(4):
-        for u in range(8):
-            inst = mm(T["psg%d" % c][:, 0:128], T.x0[32 * c:32 * c + 8, u:1024:8],
-                      T.gm0[32 * c:32 * c + 8, 128 * u:128 * u + 128], u == 0, u == 7)
-        p_g.append(done("p", inst))
+    t_own = handover(0, p_g)
+    clear("g", 0)
+
+    need("v", t_wire)
+    c_wf = copy("v", T.wf[:], T.wi[:])
     for e in range(1, 4):
         c_d = ts(T.diag[:, 128 * e:128 * e + 128], T.rowq[:], pc, T.gf[:, e:e + 1], Op.is_equal, Op.mult)
-    need("v", t_wire)
-    c_wf = vcopy(T.wf[:], T.wi[:])
-    need("v", i_rowa, i_row16, c_p7, c_p3, c_wf)
+    need("v", i_rowa, i_row16, i_cv, c_wf)
     c_am = ts(T.amat[:], T.rowa[:], T.p7f[:, 0:1], None, Op.is_equal)
     for l in range(4):
         c_bm = ts(T.bmat[:, 16 * l:16 * l + 16], T.row16[:], T.p3f[:, 0:1], T.wf[:, l:l + 1], Op.is_equal, Op.mult)
-    ev = [evac("v", 0, 0, p_g[0]), evac("s", 0, 1, p_g[1]), evac("v", 0, 2, p_g[2]), evac("s", 0, 3, p_g[3])]
-    send(0, *ev)
-    t_own = own(0, *ev)
-
     need("p", c_am, c_bm, c_d)
-    p_w = done("p", mm(T.psw[:, 0:64], T.amat[:], T.bmat[:], True, True))
     p_b = done("p", mm(T.psm[:, 128:512], T.ones[:], T.diag[:, 128:512], True, True))
+    p_w = done("p", mm(T.psw[:, 0:64], T.amat[:], T.bmat[:], True, True))
     need("s", p_b)
-    s_b = scopy(T.giveb[:, 128:512], T.psm[:, 128:512])
-    need("v", p_w, c_hc)
+    s_b = copy("s", T.giveb[:, 128:512], T.psm[:, 128:512])
+    x1 = ts(T.cvj[:], T.cvi[:], 15, None, Op.bitwise_and)
+    for k, (m, a) in enumerate(((2.0, 0.0), (2.0, 1.0), (1.0, 0.0), (1.0, 2.0))):
+        c_hc = ts(T.hc[:, k:k + 1], T.hi[:], m, a, Op.mult, Op.add)
+    ts(T.pmat[:, 0:128], T.rowq[:], pc, 64.0, Op.is_equal, Op.mult)
+    c_perm1 = ts(T.pmat[:, 128:256], T.rowq[:], pc, None, Op.is_equal)
+    need("v", x1, c_hc)
+    c_cv = ts(T.cvf[:], T.cvj[:], -1000.0, pc, Op.mult, Op.add)
+    need("v", p_w)
     for c2 in range(2):
         lst = T["lst%d" % c2]
         ts(lst[:, 0:48], T.psw[:, 0:48], 4.0, T.hc[:, c2:c2 + 1], Op.mult, Op.add)
@@ -221,48 +213,38 @@ def rank_program(g, core, T, topo):
     gm = {}
 
     def build_g(e):
+        odd = 1 if e == 2 else 0
         need("v", s_b, c_cv)
         for u in range(8):
-            gm[e] = ts(T["gm%d" % e][:, 128 * u:128 * u + 128], T.giveb[:, 128 * e:128 * e + 128], T.cvf[:, u:u + 1], None, Op.is_equal)
-
-    zero = []
-
-    def clear(k):
-        zero.append(done("v", g.vector.memset(T.tab3[:, 2048 * k:2048 * k + 2048], 0.0)))
+            gm[e] = ts(T["gm%d" % e][:, 128 * u:128 * u + 128], T.giveb[:, 128 * e:128 * e + 128], float(odd),
+                       T.cvf[:, 8 * odd + u:8 * odd + u + 1], Op.add, Op.is_equal)
 
     build_g(1)
-    clear(0)
-
     perms = {0: c_perm1, 1: c_perm1}
-    sig = [2 * (k & 7) + (k >> 3) for k in range(16)]
-    looks = []
 
     for e in range(D):
         last = e == D - 1
         arr = ("arr%d" % e, 2 * len(others))
-        land, tab = T["land%d" % e], T["tab%d" % (0, 1, 0, 3)[e]]
-        need("v", arr, t_own, c_l)
-        v_sel = vcopy(T.sel0[:], land[:, 0:512].indirect(T.lst0[:, 16 * e:16 * e + 16]))
-        need("s", arr, t_own, c_l)
-        s_sel = scopy(T.sel1[:], land[:, 0:512].indirect(T.lst1[:, 16 * e:16 * e + 16]))
-        if not last:
-            need("y", arr)
-            lo = (e + 1) * W
-            if e == 0:
-                dma("y", T.tab1[0::2, :], T.tb[:, lo:lo + W], "dt1")
-                t_tab[1] = dma("y", T.tab1[1::2, :], T.tb[:, lo:lo + W], "dt1")
-            elif e == 1:
-                need("y", *looks)
-                t_tab[2] = dma("y", T.tab0[0::2, :], T.tb[:, lo:lo + W], "dt2")
-            else:
-                need("y", *zero)
-                dma("y", T.tab3[0::4, 0:4096], T.tb[:, lo:lo + W // 2], "dt3")
-                t_tab[3] = dma("y", T.tab3[2::4, 4096:8192], T.tb[:, lo + W // 2:lo + W], "dt3")
+        land, tab = T["land%d" % e], T["tab%d" % (0, 0, 1, 3)[e]]
+        sels = []
+        for c2, q in enumerate("vs"):
+            need(q, arr, t_own, c_l)
+            sels.append(copy(q, T["sel%d" % c2][:], land[:, 0:512].indirect(T["lst%d" % c2][:, 16 * e:16 * e + 16])))
+        need("y", arr)
+        lo = 3 * W
+        if e == 0:
+            dma("y", T.tab1[0::2, :], T.tb[:, 2 * W:3 * W], "dt1")
+        elif e == 1:
+            t_tab[2] = dma("y", T.tab1[1::2, :], T.tb[:, 2 * W:3 * W], "dt1")
+        elif e == 2:
+            need("y", *zero)
+            dma("y", T.tab3[0::4, 0:4096], T.tb[:, lo:lo + W // 2], "dt3")
+            t_tab[3] = dma("y", T.tab3[2::4, 4096:8192], T.tb[:, lo + W // 2:lo + W], "dt3")
         pk = (0, 0, 256, 512)[e]
         pa = []
         need("p", perms[e])
-        for c2, tok in ((0, v_sel), (1, s_sel)):
-            need("p", tok)
+        for c2 in range(2):
+            need("p", sels[c2])
             sel, ps = T["sel%d" % c2], T["psa%d" % c2]
             mm(ps[:, 0:128], sel[:, 0:128], T.pmat[:, pk:pk + 128], True, False)
             pa.append(done("p", mm(ps[:, 0:128], sel[:, 128:256], T.pmat[:, pk + 128:pk + 256], False, True)))
@@ -271,13 +253,12 @@ def rank_program(g, core, T, topo):
         def address(c2):
             need("v", pa[c2])
             o, i = T.offs[:, 128 * c2:128 * c2 + 128], T["psa%d" % c2][:, 0:128]
-            off.append(ts(o, i, T.u2f[:, 0:1], None, Op.add) if last else vcopy(o, i))
+            off.append(ts(o, i, T.u2f[:, 0:1], None, Op.add) if last else copy("v", o, i))
 
         def look(q, a, b):
             need(q, t_tab[e], off[0 if b <= 128 else 1])
             win = tab[:, 0:8192 if last else 4096].indirect(T.offs[:, a:b])
-            out = T.rr[:, 16 * a:16 * b]
-            return vcopy(out, win) if q == "v" else scopy(out, win)
+            return copy(q, T.rr[:, 16 * a:16 * b], win)
 
         if last:
             need("v", c_u2)
@@ -296,7 +277,6 @@ def rank_program(g, core, T, topo):
             vt.append(look("v", a, b))
         for j, (a, b, c) in enumerate(cut):
             st.append(look("s", b, c))
-        looks = [vt[-1], st[-1]]
         if not last:
             p_g = []
             for j in range(4):
@@ -305,54 +285,46 @@ def rank_program(g, core, T, topo):
                     inst = mm(T["psg%d" % j][:, 0:128], T.rr[:, 1024 * j + u:1024 * j + 1024:8],
                               T["gm%d" % (e + 1)][:, 128 * u:128 * u + 128], u == 0, u == 7)
                 p_g.append(done("p", inst))
-            ev = [evac("v", e + 1, 0, p_g[0]), evac("v", e + 1, 1, p_g[1]), evac("s", e + 1, 2, p_g[2]), evac("s", e + 1, 3, p_g[3])]
-            send(e + 1, *ev)
-            t_own = own(e + 1, *ev)
+            t_own = handover(e + 1, p_g)
             if e == 0:
+                clear("g", 1)
                 build_g(2)
-                clear(1)
-                clear(2)
+                clear("v", 2)
             elif e == 1:
                 build_g(3)
                 need("v", i_rho3, i_rho4)
                 for k, rho in ((256, T.rho3), (512, T.rho4)):
                     ts(T.pmat[:, k:k + 128], rho[:], pc, 64.0, Op.is_equal, Op.mult)
-                    c_p = ts(T.pmat[:, k + 128:k + 256], rho[:], pc, None, Op.is_equal)
-                perms[2] = perms[3] = c_p
-                clear(3)
+                    perms[2] = perms[3] = ts(T.pmat[:, k + 128:k + 256], rho[:], pc, None, Op.is_equal)
+                clear("v", 3)
             else:
                 need("v", i_k4, i_z)
-                x1 = ts(T.k4j[:], T.k4i[:], 13, None, Op.bitwise_and)
-                x2 = ts(T.g16i[:], T.pint[:], 112, None, Op.bitwise_and)
-                x3 = ts(T.u2i[:], T.pint[:], 2, 1, Op.arith_shift_right, Op.bitwise_and)
-                need("v", x1, x2, x3)
-                x4 = vcopy(T.g16f[:], T.g16i[:])
+                ts(T.k4j[:], T.k4i[:], 13, None, Op.bitwise_and)
+                bits("g16", 0, 112)
+                x1 = bits("u2", 2, 1)
+                need("v", x1)
+                x2 = copy("v", T.g16f[:], T.g16i[:])
                 c_u2 = ts(T.u2f[:], T.u2i[:], 4096.0, None, Op.mult)
-                need("v", x4)
-                x5 = ts(T.k4f[:], T.k4j[:], -1000.0, T.g16f[:, 0:1], Op.mult, Op.add)
-                need("v", x5)
+                need("v", x2)
+                x3 = ts(T.k4f[:], T.k4j[:], -1000.0, T.g16f[:, 0:1], Op.mult, Op.add)
+                need("v", x3)
                 for v in range(4):
                     c_base = ts(T.base[:, 144 * v:144 * v + 144], T.zrow[:], T.k4f[:, v:v + 1], None, Op.is_equal)
         else:
             need("p", c_base)
-            blocks = []
-            for j, (a, b, c) in enumerate(pieces):
-                blocks += [(k, vt[j]) for k in range(a, b)] + [(k, st[j]) for k in range(b, c)]
             p_y = {}
-            for n, (k, tok) in enumerate(blocks):
-                need("p", tok)
-                z = 15 - sig[k]
-                for v in range(4):
-                    inst = mm(T["psg%d" % v][:, 0:64], T.base[:, 144 * v + z:144 * v + z + 128],
-                              T.rr[:, 256 * k + v:256 * k + 256:4], n == 0, n == len(blocks) - 1)
-                    if n == len(blocks) - 1:
-                        p_y[v] = done("p", inst)
+            for j, (x, y, z) in enumerate(pieces):
+                for s in range(x, z):
+                    need("p", vt[j] if s < y else st[j])
+                    for v in range(4):
+                        at = 144 * v + 15 - s
+                        inst = mm(T["psg%d" % v][:, 0:64], T.base[:, at:at + 128], T.rr[:, 256 * s + v:256 * s + 256:4], s == 0, s == 15)
+                        if s == 15:
+                            p_y[v] = done("p", inst)
             fin = []
-            for v, q in ((0, "v"), (1, "s"), (2, "v"), (3, "s")):
+            for v, q in enumerate("vsvs"):
                 need(q, p_y[v])
-                out, in_ = T.ysb[:, v:256:4], T["psg%d" % v][:, 0:64]
-                fin.append(vcopy(out, in_) if q == "v" else scopy(out, in_))
+                fin.append(copy(q, T.ysb[:, v:256:4], T["psg%d" % v][:, 0:64]))
             need("y", *fin)
-            t_y = dma("y", T.y[:, :], T.ysb[:], "dy")
-            need("y", t_y)
+            need("y", dma("y", T.y[:, :], T.ysb[:], "dy"))
     need("g", *[(n, count[n]) for n in ("qv", "qs", "qp", "qg", "loc")])

@@ -5,21 +5,25 @@ BF, F32, I32, U16 = "bfloat16", "float32", "int32", "uint16"
 D = 4
 
 SCRATCH = {}
-for _t, _names in ((BF, "xb 256 xt 256 xr 256 diag 512 giveb 512 sel0 256 sel1 256 rr 4096 tab0 4096 tab1 4096 tab3 8192 rowq 128 "
-                        "rowa 128 row16 16 rho3 128 rho4 128 zrow 144 ones 128 amat 128 bmat 64 base 576 pmat 768 "
-                        "gm0 1024 gm1 1024 gm2 1024 gm3 1024 sb0 512 sb1 512 sb2 512 sb3 512 land0 512 land1 512 land2 512 land3 512"),
-                   (F32, "gf 4 wf 4 ysb 256 pcol 1 v0f 4 cvf 16 k4f 4 hc 4 kap 1 g16f 1 p7f 1 p3f 1 hf 1 u2f 1 p96f 1 taf 1 tauf 1"),
+for _t, _names in ((BF, "xb 256 xt 256 xr 256 diag 512 giveb 512 sel0 128 sel1 128 sel2 128 sel3 128 rr0 2048 rr1 2048 "
+                        "tab0 4096 tab1 4096 tab3 8192 rowq 128 rowa 128 row16 16 rho3 128 rho4 128 zrow 144 ones 128 amat 128 "
+                        "bmat 64 base 576 pmat 768 gm0 1024 gm1 1024 gm2 1024 gm3 1024"),
+                   (F32, "gf 4 wf 4 ysb 256 pcol 1 v0f 4 cvf 16 k4f 4 kap 1 g16f 1 p7f 1 p3f 1 hf 1 u2f 1 p96f 1 taf 1 tauf 1"),
                    (I32, "xi 256 gi 4 wi 4 pint 1 v0i 4 v0j 4 cvi 16 cvj 16 k4i 4 k4j 4 xli 16 g16i 1 p7i 1 p3i 1 hi 1 u2i 1 "
                          "p96i 1 tai 1 taui 1"),
-                   (U16, "offs 256 lst0 64 lst1 64 xl 16")):
+                   (U16, "offs0 128 offs1 128 lst 64 xl 16")):
     _w = _names.split()
     for _k in range(0, len(_w), 2):
         SCRATCH[_w[_k]] = ("sbuf", [128, int(_w[_k + 1])], _t)
+for _e in range(4):
+    for _b in range(2):
+        SCRATCH["sb%d%d" % (_e, _b)] = ("sbuf", [128, 256], BF)
+        SCRATCH["land%d%d" % (_e, _b)] = ("sbuf", [128, 256], BF)
 for _n in ("psg0", "psg1", "psg2", "psg3", "psa0", "psa1", "psm", "psw"):
     SCRATCH[_n] = ("psum", [128, 512], F32)
 
-SEMAPHORES = ["qv", "qs", "qp", "qg", "loc", "arr0", "arr1", "arr2", "arr3",
-              "dgive", "dwire", "dx", "dt0", "dt1", "dt3", "dy"]
+SEMAPHORES = ["qv", "qs", "qp", "qg", "loc", "dgive", "dwire", "dx", "dt0", "dt1", "dt3", "dz", "dy"]
+SEMAPHORES += ["arr%d%d" % (_e, _b) for _e in range(4) for _b in range(2)]
 
 
 def rank_program(g, core, T, topo):
@@ -82,7 +86,7 @@ def rank_program(g, core, T, topo):
 
     i_pint = iota(T.pint[:], [[0, 1]], 0, 1, True)
     i_pcol = iota(T.pcol[:], [[0, 1]], 0, 1)
-    i_xl = iota(T.xli[:], [[16, 2], [32, 2], [4, 4]], 0, 0, True)
+    i_xl = iota(T.xli[:], [[8, 4], [32, 2], [4, 2]], 0, 0, True)
     i_v0 = iota(T.v0i[:], [[-8, 4]], 0, 1, True)
     i_rowq = iota(T.rowq[:], [[1, 128]], 0, 0)
     i_cv = iota(T.cvi[:], [[-1, 2], [-2, 8]], 0, 1, True)
@@ -94,9 +98,13 @@ def rank_program(g, core, T, topo):
     i_z = iota(T.zrow[:], [[16, 9], [-1000, 16]], 15000, 0)
     zero = []
 
-    def clear(q, k):
-        part = T.tab3[:, 2048 * k:2048 * k + 2048]
-        zero.append(iota(part, [[0, 2048]], 0, 0) if q == "g" else done("v", g.vector.memset(part, 0.0)))
+    def clear(q, a, b):
+        part = T.tab3[:, a:b]
+        if q == "g":
+            zero.append(iota(part, [[0, b - a]], 0, 0))
+        else:
+            need("s", t_tab[0])
+            zero.append(done("s", g.scalar.activation(part, T.tab0[:, 0:b - a], Copy, scale=0.0)))
 
     pc = T.pcol[:, 0:1]
     c_ones = done("v", g.vector.memset(T.ones[:], 1.0))
@@ -110,8 +118,8 @@ def rank_program(g, core, T, topo):
     for n, sh, mk in (("ta", 2, 3), ("tau", 0, 3), ("p7", 0, 7), ("p96", 0, 96), ("p3", 3, 15), ("h", 3, 1)):
         x1 = bits(n, sh, mk)
     need("v", x1)
-    for n in ("ta", "p7", "p96", "p3"):
-        copy("v", T[n + "f"][:], T[n + "i"][:])
+    for n in ("ta", "p7", "p96", "p3", "h"):
+        x1 = copy("v", T[n + "f"][:], T[n + "i"][:])
     need("v", i_v0, i_xl)
     x2 = ts(T.v0j[:], T.v0i[:], 24, None, Op.bitwise_and)
     need("v", x2)
@@ -120,7 +128,13 @@ def rank_program(g, core, T, topo):
     need("v", x3)
     c_xl = ts(T.xl[:], T.xli[:], T.tauf[:, 0:1], None, Op.add)
     c_v0 = ts(T.v0f[:], T.v0j[:], -1000.0, T.kap[:, 0:1], Op.mult, Op.add)
-    need("v", i_rowq)
+    need("v", i_rowq, i_rowa, i_cv)
+    x1 = ts(T.cvj[:], T.cvi[:], 15, None, Op.bitwise_and)
+    ts(T.pmat[:, 0:128], T.rowq[:], pc, 64.0, Op.is_equal, Op.mult)
+    c_perm1 = ts(T.pmat[:, 128:256], T.rowq[:], pc, None, Op.is_equal)
+    c_am = ts(T.amat[:], T.rowa[:], T.p7f[:, 0:1], None, Op.is_equal)
+    need("v", x1)
+    c_cv = ts(T.cvf[:], T.cvj[:], -1000.0, pc, Op.mult, Op.add)
 
     need("v", t_give)
     c_gf = ts(T.gf[:], T.gi[:], 2.0, None, Op.mult)
@@ -139,19 +153,15 @@ def rank_program(g, core, T, topo):
         need(q, c_xt, c_xl)
         xr.append(copy(q, T.xr[:, 128 * k:128 * k + 128], T.xt[:, 0:256].indirect(T.xl[:, 8 * k:8 * k + 8])))
     need("v", s_b0, c_v0)
-    need("p", *xr)
-    p_g = []
-    for c in range(4):
+    g0 = {}
+    for idx in range(4):
         for g2 in range(2):
-            k = 2 * c + g2
-            tok = ts(T.gm0[:, 128 * k:128 * k + 128], T.giveb[:, 0:128], -16.0 * g2, T.v0f[:, c:c + 1], Op.add, Op.is_equal)
-            need("p", tok)
-            inst = mm(T["psg%d" % c][:, 0:128], T.xr[:, 128 * g2:128 * g2 + 128], T.gm0[:, 128 * k:128 * k + 128], g2 == 0, g2 == 1)
-        p_g.append(done("p", inst))
+            k = 2 * idx + g2
+            g0[k] = ts(T.gm0[:, 128 * k:128 * k + 128], T.giveb[:, 0:128], -16.0 * g2, T.v0f[:, idx:idx + 1], Op.add, Op.is_equal)
 
     others = [r for r in range(N) if r != rank]
 
-    def send(e, *tokens):
+    def send(e, b, *tokens):
         need("g", *tokens)
         pools = [[], []]
         for k, en in enumerate(topo.engines(core, cores[others[0]])):
@@ -167,30 +177,44 @@ def rank_program(g, core, T, topo):
                 mask |= 1 << pool.pop(0)
             rid, pid = topo.addr(dst)[:2]
             moves.append(RemoteDMATransfer(dst_ids=[DstId(rid=rid, pnc=pid)], dma_engine_mask=mask,
-                                           remote_sem=T.sem["arr%d" % e],
-                                           src=T["sb%d" % e][:, 64 * r:64 * r + 64],
-                                           dst=T["land%d" % e][:, 64 * rank:64 * rank + 64]))
+                                           remote_sem=T.sem["arr%d%d" % (e, b)],
+                                           src=T["sb%d%d" % (e, b)][:, 32 * r:32 * r + 32],
+                                           dst=T["land%d%d" % (e, b)][:, 32 * rank:32 * rank + 32]))
         g.remote_dma_fused(moves, local_sem=T.sem["loc"])
         count["loc"] = count.get("loc", 0) + 2 * len(others)
 
-    def handover(e, p_g):
-        ev = []
-        for c, q in enumerate("vvss" if e else "vsvs"):
-            need(q, p_g[c])
-            ev.append(copy(q, T["sb%d" % e][:, c:512:4], T["psg%d" % c][:, 0:128]))
-        send(e, *ev)
-        need("v", *ev)
-        return copy("v", T["land%d" % e][:, 64 * rank:64 * rank + 64], T["sb%d" % e][:, 64 * rank:64 * rank + 64])
+    def evac(q, e, b, c, tok):
+        need(q, tok)
+        return copy(q, T["sb%d%d" % (e, b)][:, c:256:2], T["psg%d" % (2 * b + c)][:, 0:128])
 
-    t_own = handover(0, p_g)
-    clear("g", 0)
+    t_own = {}
+
+    def own(e, b, tokens):
+        need("v", *tokens)
+        t_own[(e, b)] = copy("v", T["land%d%d" % (e, b)][:, 32 * rank:32 * rank + 32], T["sb%d%d" % (e, b)][:, 32 * rank:32 * rank + 32])
+
+    need("p", *xr)
+    evs = []
+    for b in range(2):
+        p_g = []
+        for c in range(2):
+            for z in range(2):
+                for g2 in range(2):
+                    k = 2 * (2 * c + z) + g2
+                    need("p", g0[k])
+                    inst = mm(T["psg%d" % (2 * b + c)][64 * z:64 * z + 64, 0:128], T.xr[:, 64 * (2 * g2 + b):64 * (2 * g2 + b) + 64],
+                              T.gm0[:, 128 * k:128 * k + 128], g2 == 0, g2 == 1)
+            p_g.append(done("p", inst))
+        ev = [evac("v", 0, b, 0, p_g[0]), evac("s", 0, b, 1, p_g[1])]
+        send(0, b, *ev)
+        evs.append(ev)
+    clear("g", 0, 3072)
 
     need("v", t_wire)
     c_wf = copy("v", T.wf[:], T.wi[:])
     for e in range(1, 4):
         c_d = ts(T.diag[:, 128 * e:128 * e + 128], T.rowq[:], pc, T.gf[:, e:e + 1], Op.is_equal, Op.mult)
-    need("v", i_rowa, i_row16, i_cv, c_wf)
-    c_am = ts(T.amat[:], T.rowa[:], T.p7f[:, 0:1], None, Op.is_equal)
+    need("v", i_row16, c_wf)
     for l in range(4):
         c_bm = ts(T.bmat[:, 16 * l:16 * l + 16], T.row16[:], T.p3f[:, 0:1], T.wf[:, l:l + 1], Op.is_equal, Op.mult)
     need("p", c_am, c_bm, c_d)
@@ -198,18 +222,10 @@ def rank_program(g, core, T, topo):
     p_w = done("p", mm(T.psw[:, 0:64], T.amat[:], T.bmat[:], True, True))
     need("s", p_b)
     s_b = copy("s", T.giveb[:, 128:512], T.psm[:, 128:512])
-    x1 = ts(T.cvj[:], T.cvi[:], 15, None, Op.bitwise_and)
-    for k, (m, a) in enumerate(((2.0, 0.0), (2.0, 1.0), (1.0, 0.0), (1.0, 2.0))):
-        c_hc = ts(T.hc[:, k:k + 1], T.hi[:], m, a, Op.mult, Op.add)
-    ts(T.pmat[:, 0:128], T.rowq[:], pc, 64.0, Op.is_equal, Op.mult)
-    c_perm1 = ts(T.pmat[:, 128:256], T.rowq[:], pc, None, Op.is_equal)
-    need("v", x1, c_hc)
-    c_cv = ts(T.cvf[:], T.cvj[:], -1000.0, pc, Op.mult, Op.add)
+    for b in range(2):
+        own(0, b, evs[b])
     need("v", p_w)
-    for c2 in range(2):
-        lst = T["lst%d" % c2]
-        ts(lst[:, 0:48], T.psw[:, 0:48], 4.0, T.hc[:, c2:c2 + 1], Op.mult, Op.add)
-        c_l = ts(lst[:, 48:64], T.psw[:, 48:64], 4.0, T.hc[:, 2 + c2:3 + c2], Op.mult, Op.add)
+    c_l = ts(T.lst[:], T.psw[:, 0:64], 2.0, T.hf[:, 0:1], Op.mult, Op.add)
     gm = {}
 
     def build_g(e):
@@ -220,111 +236,145 @@ def rank_program(g, core, T, topo):
                        T.cvf[:, 8 * odd + u:8 * odd + u + 1], Op.add, Op.is_equal)
 
     build_g(1)
+    clear("s", 3072, 4096)
+
     perms = {0: c_perm1, 1: c_perm1}
+    y_banks = [T.psm, T.psw, T.psg0, T.psg1]
 
     for e in range(D):
         last = e == D - 1
-        arr = ("arr%d" % e, 2 * len(others))
-        land, tab = T["land%d" % e], T["tab%d" % (0, 0, 1, 3)[e]]
-        sels = []
-        for c2, q in enumerate("vs"):
-            need(q, arr, t_own, c_l)
-            sels.append(copy(q, T["sel%d" % c2][:], land[:, 0:512].indirect(T["lst%d" % c2][:, 16 * e:16 * e + 16])))
-        need("y", arr)
-        lo = 3 * W
+        tab = T["tab%d" % (0, 0, 1, 3)[e]]
+        pk = (0, 0, 256, 512)[e]
+        sel, pa, off = {}, {}, {}
+        tok = {}
+        pieces = {}
+        for b in range(2):
+            pieces[b], at = [], 0
+            for n in ((2, 1, 1) if last or b == 0 else (2, 2)):
+                pieces[b].append((at, at + n, at + 2 * n))
+                at += 2 * n
+
+        def pick(q, b):
+            i = 0 if q == "v" else 1
+            need(q, ("arr%d%d" % (e, b), 2 * len(others)), t_own[(e, b)], c_l)
+            sel[(q, b)] = copy(q, T["sel%d" % (2 * b + i)][:], T["land%d%d" % (e, b)][:, 0:256].indirect(T.lst[:, 16 * e + 8 * i:16 * e + 8 * i + 8]))
+
+        def turn(b):
+            for i, q in enumerate("vs"):
+                need("p", perms[e], sel[(q, b)])
+                inst = mm(T["psa%d" % b][:, 0:128], T["sel%d" % (2 * b + i)][:], T.pmat[:, pk + 128 * i:pk + 128 * i + 128], i == 0, i == 1)
+            pa[b] = done("p", inst)
+
+        def cast(b):
+            need("v", pa[b])
+            o, i = T["offs%d" % b][:], T["psa%d" % b][:, 0:128]
+            off[b] = ts(o, i, T.u2f[:, 0:1], None, Op.add) if last else copy("v", o, i)
+
+        def look(q, b, j):
+            x, y, z = pieces[b][j]
+            lo, hi = (x, y) if q == "v" else (y, z)
+            need(q, t_tab[e], off[b])
+            win = tab[:, 0:8192 if last else 4096].indirect(T["offs%d" % b][:, 16 * lo:16 * hi])
+            tok[(q, b, j)] = copy(q, T["rr%d" % b][:, 256 * lo:256 * hi], win)
+
+        def give(b, c):
+            hit = [k for k in range(len(pieces[b])) if pieces[b][k][2] == 4 * c + 4][0]
+            need("p", tok[("v", b, hit)], tok[("s", b, hit)], gm[e + 1])
+            for u in range(8):
+                inst = mm(T["psg%d" % (2 * b + c)][:, 0:128], T["rr%d" % b][:, 1024 * c + u:1024 * c + 1024:8],
+                          T["gm%d" % (e + 1)][:, 128 * u:128 * u + 128], u == 0, u == 7)
+            return done("p", inst)
+
+        p_y = {}
+
+        def place(b, j):
+            x, y, z = pieces[b][j]
+            for k in range(x, z):
+                need("p", tok[("v" if k < y else "s", b, j)])
+                s = 8 * b + k
+                for v in range(4):
+                    at = 144 * v + 15 - s
+                    inst = mm(y_banks[v][:, 0:64], T.base[:, at:at + 128], T["rr%d" % b][:, 256 * k + v:256 * k + 256:4], s == 0, s == 15)
+                    if s == 15:
+                        p_y[v] = done("p", inst)
+
+        for q in "vs":
+            pick(q, 0)
+        turn(0)
+        if last:
+            need("v", c_u2)
+            need("p", c_base)
+        cast(0)
+        for k in range(3):
+            if k == 2:
+                for q in "vs":
+                    pick(q, 1)
+            for q in "vs":
+                look(q, 0, k)
+        if last:
+            place(0, 0)
+            turn(1)
+            place(0, 1)
+            place(0, 2)
+            cast(1)
+        else:
+            p0 = [give(0, 0)]
+            turn(1)
+            p0.append(give(0, 1))
+            cast(1)
+            ev0 = [evac("v", e + 1, 0, 0, p0[0])]
+        for k in range(len(pieces[1])):
+            for q in "vs":
+                look(q, 1, k)
+            if k == 0 and not last:
+                ev0.append(evac("s", e + 1, 0, 1, p0[1]))
+                send(e + 1, 0, *ev0)
+        need("y", ("arr%d1" % e, 2 * len(others)))
         if e == 0:
             dma("y", T.tab1[0::2, :], T.tb[:, 2 * W:3 * W], "dt1")
         elif e == 1:
             t_tab[2] = dma("y", T.tab1[1::2, :], T.tb[:, 2 * W:3 * W], "dt1")
+            need("y", *zero)
+            zero.append(dma("y", T.tab3[:, 6144:8192], T.tab3[:, 0:2048], "dz"))
         elif e == 2:
             need("y", *zero)
-            dma("y", T.tab3[0::4, 0:4096], T.tb[:, lo:lo + W // 2], "dt3")
-            t_tab[3] = dma("y", T.tab3[2::4, 4096:8192], T.tb[:, lo + W // 2:lo + W], "dt3")
-        pk = (0, 0, 256, 512)[e]
-        pa = []
-        need("p", perms[e])
-        for c2 in range(2):
-            need("p", sels[c2])
-            sel, ps = T["sel%d" % c2], T["psa%d" % c2]
-            mm(ps[:, 0:128], sel[:, 0:128], T.pmat[:, pk:pk + 128], True, False)
-            pa.append(done("p", mm(ps[:, 0:128], sel[:, 128:256], T.pmat[:, pk + 128:pk + 256], False, True)))
-        off = []
-
-        def address(c2):
-            need("v", pa[c2])
-            o, i = T.offs[:, 128 * c2:128 * c2 + 128], T["psa%d" % c2][:, 0:128]
-            off.append(ts(o, i, T.u2f[:, 0:1], None, Op.add) if last else copy("v", o, i))
-
-        def look(q, a, b):
-            need(q, t_tab[e], off[0 if b <= 128 else 1])
-            win = tab[:, 0:8192 if last else 4096].indirect(T.offs[:, a:b])
-            return copy(q, T.rr[:, 16 * a:16 * b], win)
-
+            dma("y", T.tab3[0::4, 0:4096], T.tb[:, 3 * W:3 * W + W // 2], "dt3")
+            t_tab[3] = dma("y", T.tab3[2::4, 4096:8192], T.tb[:, 3 * W + W // 2:4 * W], "dt3")
         if last:
-            need("v", c_u2)
-            pieces, at = [], 0
-            for n in (2, 2, 2, 1, 1):
-                pieces.append((at, at + n, at + 2 * n))
-                at += 2 * n
-            cut = [(16 * a, 16 * b, 16 * c) for a, b, c in pieces]
+            for k in range(len(pieces[1])):
+                place(1, k)
+            break
+        p1 = [give(1, c) for c in range(2)]
+        own(e + 1, 0, ev0)
+        ev1 = [evac("v", e + 1, 1, 0, p1[0]), evac("s", e + 1, 1, 1, p1[1])]
+        send(e + 1, 1, *ev1)
+        if e == 0:
+            clear("g", 4096, 6144)
+            build_g(2)
+        elif e == 1:
+            build_g(3)
+            need("v", i_rho3, i_rho4)
+            for k, rho in ((256, T.rho3), (512, T.rho4)):
+                ts(T.pmat[:, k:k + 128], rho[:], pc, 64.0, Op.is_equal, Op.mult)
+                perms[2] = perms[3] = ts(T.pmat[:, k + 128:k + 256], rho[:], pc, None, Op.is_equal)
         else:
-            cut = [(64 * j, 64 * j + 30, 64 * j + 64) for j in range(4)]
-        address(0)
-        vt, st = [], []
-        for j, (a, b, c) in enumerate(cut):
-            if j == 1:
-                address(1)
-            vt.append(look("v", a, b))
-        for j, (a, b, c) in enumerate(cut):
-            st.append(look("s", b, c))
-        if not last:
-            p_g = []
-            for j in range(4):
-                need("p", vt[j], st[j], gm[e + 1])
-                for u in range(8):
-                    inst = mm(T["psg%d" % j][:, 0:128], T.rr[:, 1024 * j + u:1024 * j + 1024:8],
-                              T["gm%d" % (e + 1)][:, 128 * u:128 * u + 128], u == 0, u == 7)
-                p_g.append(done("p", inst))
-            t_own = handover(e + 1, p_g)
-            if e == 0:
-                clear("g", 1)
-                build_g(2)
-                clear("v", 2)
-            elif e == 1:
-                build_g(3)
-                need("v", i_rho3, i_rho4)
-                for k, rho in ((256, T.rho3), (512, T.rho4)):
-                    ts(T.pmat[:, k:k + 128], rho[:], pc, 64.0, Op.is_equal, Op.mult)
-                    perms[2] = perms[3] = ts(T.pmat[:, k + 128:k + 256], rho[:], pc, None, Op.is_equal)
-                clear("v", 3)
-            else:
-                need("v", i_k4, i_z)
-                ts(T.k4j[:], T.k4i[:], 13, None, Op.bitwise_and)
-                bits("g16", 0, 112)
-                x1 = bits("u2", 2, 1)
-                need("v", x1)
-                x2 = copy("v", T.g16f[:], T.g16i[:])
-                c_u2 = ts(T.u2f[:], T.u2i[:], 4096.0, None, Op.mult)
-                need("v", x2)
-                x3 = ts(T.k4f[:], T.k4j[:], -1000.0, T.g16f[:, 0:1], Op.mult, Op.add)
-                need("v", x3)
-                for v in range(4):
-                    c_base = ts(T.base[:, 144 * v:144 * v + 144], T.zrow[:], T.k4f[:, v:v + 1], None, Op.is_equal)
-        else:
-            need("p", c_base)
-            p_y = {}
-            for j, (x, y, z) in enumerate(pieces):
-                for s in range(x, z):
-                    need("p", vt[j] if s < y else st[j])
-                    for v in range(4):
-                        at = 144 * v + 15 - s
-                        inst = mm(T["psg%d" % v][:, 0:64], T.base[:, at:at + 128], T.rr[:, 256 * s + v:256 * s + 256:4], s == 0, s == 15)
-                        if s == 15:
-                            p_y[v] = done("p", inst)
-            fin = []
-            for v, q in enumerate("vsvs"):
-                need(q, p_y[v])
-                fin.append(copy(q, T.ysb[:, v:256:4], T["psg%d" % v][:, 0:64]))
-            need("y", *fin)
-            need("y", dma("y", T.y[:, :], T.ysb[:], "dy"))
+            need("v", i_k4, i_z)
+            ts(T.k4j[:], T.k4i[:], 13, None, Op.bitwise_and)
+            bits("g16", 0, 112)
+            x1 = bits("u2", 2, 1)
+            need("v", x1)
+            x2 = copy("v", T.g16f[:], T.g16i[:])
+            c_u2 = ts(T.u2f[:], T.u2i[:], 4096.0, None, Op.mult)
+            need("v", x2)
+            x3 = ts(T.k4f[:], T.k4j[:], -1000.0, T.g16f[:, 0:1], Op.mult, Op.add)
+            need("v", x3)
+            for v in range(4):
+                c_base = ts(T.base[:, 144 * v:144 * v + 144], T.zrow[:], T.k4f[:, v:v + 1], None, Op.is_equal)
+        own(e + 1, 1, ev1)
+    fin = []
+    for v, q in enumerate("vsvs"):
+        need(q, p_y[v])
+        fin.append(copy(q, T.ysb[:, v:256:4], y_banks[v][:, 0:64]))
+    need("y", *fin)
+    need("y", dma("y", T.y[:, :], T.ysb[:], "dy"))
     need("g", *[(n, count[n]) for n in ("qv", "qs", "qp", "qg", "loc")])

@@ -5,24 +5,23 @@ BF, F32, I32, U16 = "bfloat16", "float32", "int32", "uint16"
 D = 4
 
 SCRATCH = {}
-for _t, _names in ((BF, "xb 256 xt 256 xr 256 diag 512 giveb 512 sel0 128 sel1 128 sel2 128 sel3 128 rr0 2048 rr1 2048 "
-                        "tab0 4096 tab1 4096 tab3 8192 rowq 128 rowa 128 row16 16 rho3 128 rho4 128 zrow 144 ones 128 amat 128 "
-                        "bmat 64 base 576 pmat 768 gm0 1024 gm1 1024 gm2 1024 gm3 1024"),
-                   (F32, "gf 4 wf 4 ysb 256 pcol 1 v0f 4 cvf 16 k4f 4 kap 1 g16f 1 p7f 1 p3f 1 hf 1 u2f 1 p96f 1 taf 1 tauf 1"),
-                   (I32, "xi 256 gi 4 wi 4 pint 1 v0i 4 v0j 4 cvi 16 cvj 16 k4i 4 k4j 4 xli 16 g16i 1 p7i 1 p3i 1 hi 1 u2i 1 "
-                         "p96i 1 tai 1 taui 1"),
-                   (U16, "offs0 128 offs1 128 lst 64 xl 16")):
+for _t, _names in ((BF, "xb0 128 xb1 128 xt0 128 xt1 128 diag 512 oh 512 glb 32 gmk 32 cmpb 4 sel0 128 sel1 128 sel2 128 sel3 128 "
+                        "rr0 2048 rr1 2048 tab0 4096 tab1 4096 tab3 8192 rowq 128 rowe 128 rowa 128 row16 16 rowu 64 rows 128 "
+                        "rowm 32 mask 32 rho3 128 rho4 128 zrow 144 ones 128 amat 128 bmq 64 bmn 64 base 576 pmat 768 e0 128 "
+                        "ev 64 od 64 selb 128"),
+                   (F32, "wf 4 wqf 4 ysb0 256 ysb1 256 pcol 1 k4f 4 pf 8 hf 1 u2f 1"),
+                   (I32, "xi0 128 xi1 128 gl 32 wi 4 wqi 4 pint 1 k4i 4 k4j 4 pk 8"),
+                   (U16, "offs0 128 offs1 128 lst 64")):
     _w = _names.split()
     for _k in range(0, len(_w), 2):
         SCRATCH[_w[_k]] = ("sbuf", [128, int(_w[_k + 1])], _t)
 for _e in range(4):
     for _b in range(2):
-        SCRATCH["sb%d%d" % (_e, _b)] = ("sbuf", [128, 256], BF)
-        SCRATCH["land%d%d" % (_e, _b)] = ("sbuf", [128, 256], BF)
+        SCRATCH["land%d%d" % (_e, _b)] = ("sbuf", [128, 1024], BF)
 for _n in ("psg0", "psg1", "psg2", "psg3", "psa0", "psa1", "psm", "psw"):
     SCRATCH[_n] = ("psum", [128, 512], F32)
 
-SEMAPHORES = ["qv", "qs", "qp", "qg", "loc", "dgive", "dwire", "dx", "dt0", "dt1", "dt3", "dz", "dy"]
+SEMAPHORES = ["qv", "qs", "qp", "qg", "loc", "dgive", "dwire", "dx0", "dx1", "dt0", "dt1", "dt3", "dy", "arrg"]
 SEMAPHORES += ["arr%d%d" % (_e, _b) for _e in range(4) for _b in range(2)]
 
 
@@ -76,170 +75,252 @@ def rank_program(g, core, T, topo):
     def mm(out, lhsT, rhs, start, stop):
         return g.tensor.matmul(out, lhsT, rhs, start, stop)
 
-    t_give = dma("y", T.gi[:], T.give[:, :], "dgive")
-    t_x = dma("s", T.xi[:], T.x[:, :], "dx")
+    others = [cores[(rank + k) % N] for k in range(1, N)]
+    engines = topo.mask(core, others[0])
+    for dst in others:
+        engines &= topo.mask(core, dst)
+    n_eng = len([k for k in topo.engines(core, others[0]) if engines >> k & 1])
+    arrive = n_eng * len(others)
+
+    def send(name, arr, lo, hi, *tokens):
+        need("g", *tokens)
+        ids = [DstId(rid=topo.addr(dst)[0], pnc=topo.addr(dst)[1]) for dst in others]
+        part = T[name][:, lo:hi]
+        g.remote_dma_fused([RemoteDMATransfer(dst_ids=ids, dma_engine_mask=engines, remote_sem=T.sem[arr],
+                                              srcs=[part], dsts=[part] * len(others))], local_sem=T.sem["loc"])
+        count["loc"] = count.get("loc", 0) + n_eng
+
+    t_x = {}
+
+    def load_x(q, b, gb):
+        for z in range(2):
+            at = 128 * b + 64 * z
+            t_x[b] = dma(q, T["xi%d" % b][z::2, 64 * gb:64 * gb + 64], T.x[64 * gb:64 * gb + 64, at:at + 64], "dx%d" % b)
+
+    t_give = dma("y", T.gl[:, 4 * rank:4 * rank + 4], T.give[:, :], "dgive")
+    load_x("s", 0, 0)
+    load_x("y", 0, 1)
+    load_x("s", 1, 0)
+    load_x("y", 1, 1)
     t_wire = dma("y", T.wi[:], T.wires[:, :], "dwire")
     W = 8 * 4096
-    dma("y", T.tab0[0::2, :], T.tb[:, 0:W], "dt0")
     t_tab = {}
+    dma("y", T.tab0[0::2, :], T.tb[:, 0:W], "dt0")
     t_tab[0] = t_tab[1] = dma("y", T.tab0[1::2, :], T.tb[:, W:2 * W], "dt0")
 
-    i_pint = iota(T.pint[:], [[0, 1]], 0, 1, True)
     i_pcol = iota(T.pcol[:], [[0, 1]], 0, 1)
-    i_xl = iota(T.xli[:], [[8, 4], [32, 2], [4, 2]], 0, 0, True)
-    i_v0 = iota(T.v0i[:], [[-8, 4]], 0, 1, True)
+    i_pint = iota(T.pint[:], [[0, 1]], 0, 1, True)
+    i_rowe = iota(T.rowe[:], [[8, 4], [32, 4], [1, 8]], 0, 0)
     i_rowq = iota(T.rowq[:], [[1, 128]], 0, 0)
-    i_cv = iota(T.cvi[:], [[-1, 2], [-2, 8]], 0, 1, True)
-    i_rowa = iota(T.rowa[:], [[0, 16], [1, 8]], 0, 0)
+    i_rows = iota(T.rows[:], [[0, 8], [1, 16]], 16 * rank, 0)
+    i_rowm = iota(T.rowm[:], [[1, 8], [0, 4]], 0, 0)
     i_row16 = iota(T.row16[:], [[1, 2], [2, 8]], 0, 0)
-    i_rho3 = iota(T.rho3[:], [[1, 2], [2, 64]], 0, 0)
-    i_rho4 = iota(T.rho4[:], [[4, 32], [1, 2], [2, 2]], 0, 0)
-    i_k4 = iota(T.k4i[:], [[-4, 4]], 0, 1, True)
-    i_z = iota(T.zrow[:], [[16, 9], [-1000, 16]], 15000, 0)
-    zero = []
+    send("gl", "arrg", 4 * rank, 4 * rank + 4, t_give)
+
+    pc = T.pcol[:, 0:1]
+    zero = [done("v", g.vector.memset(T.tab3[:, 0:512], 0.0)), done("v", g.vector.memset(T.tab3[:, 512:1536], 0.0))]
 
     def clear(q, a, b):
         part = T.tab3[:, a:b]
         if q == "g":
             zero.append(iota(part, [[0, b - a]], 0, 0))
         else:
-            need("s", t_tab[0])
-            zero.append(done("s", g.scalar.activation(part, T.tab0[:, 0:b - a], Copy, scale=0.0)))
+            need("s", zero[0])
+            zero.append(copy("s", part, T.tab3[:, 0:b - a]))
 
-    pc = T.pcol[:, 0:1]
+    for k in range(3, 6):
+        clear("s", 512 * k, 512 * k + 512)
     c_ones = done("v", g.vector.memset(T.ones[:], 1.0))
-    need("v", i_pint)
+    need("v", i_pint, i_rowe)
+    c_e0 = ts(T.e0[:], T.rowe[:], pc, None, Op.is_equal)
 
-    def bits(name, shift, mask):
+    def bits(k, shift, mask):
         if shift:
-            return ts(T[name + "i"][:], T.pint[:], shift, mask, Op.arith_shift_right, Op.bitwise_and)
-        return ts(T[name + "i"][:], T.pint[:], mask, None, Op.bitwise_and)
+            return ts(T.pk[:, k:k + 1], T.pint[:], shift, mask, Op.arith_shift_right, Op.bitwise_and)
+        return ts(T.pk[:, k:k + 1], T.pint[:], mask, None, Op.bitwise_and)
 
-    for n, sh, mk in (("ta", 2, 3), ("tau", 0, 3), ("p7", 0, 7), ("p96", 0, 96), ("p3", 3, 15), ("h", 3, 1)):
-        x1 = bits(n, sh, mk)
-    need("v", x1)
-    for n in ("ta", "p7", "p96", "p3", "h"):
-        x1 = copy("v", T[n + "f"][:], T[n + "i"][:])
-    need("v", i_v0, i_xl)
-    x2 = ts(T.v0j[:], T.v0i[:], 24, None, Op.bitwise_and)
-    need("v", x2)
-    ts(T.tauf[:], T.taui[:], 64.0, T.taf[:, 0:1], Op.mult, Op.add)
-    x3 = ts(T.kap[:], T.p7f[:], 2.0, T.p96f[:, 0:1], Op.mult, Op.add)
-    need("v", x3)
-    c_xl = ts(T.xl[:], T.xli[:], T.tauf[:, 0:1], None, Op.add)
-    c_v0 = ts(T.v0f[:], T.v0j[:], -1000.0, T.kap[:, 0:1], Op.mult, Op.add)
-    need("v", i_rowq, i_rowa, i_cv)
-    x1 = ts(T.cvj[:], T.cvi[:], 15, None, Op.bitwise_and)
-    ts(T.pmat[:, 0:128], T.rowq[:], pc, 64.0, Op.is_equal, Op.mult)
-    c_perm1 = ts(T.pmat[:, 128:256], T.rowq[:], pc, None, Op.is_equal)
-    c_am = ts(T.amat[:], T.rowa[:], T.p7f[:, 0:1], None, Op.is_equal)
-    need("v", x1)
-    c_cv = ts(T.cvf[:], T.cvj[:], -1000.0, pc, Op.mult, Op.add)
+    for k, (sh, mk) in enumerate(((0, 7), (3, 15), (4, 7), (0, 8), (0, 4), (0, 112))):
+        c_i = bits(k, sh, mk)
+    p7, p3, pq, h8, u4, g16 = [T.pf[:, k:k + 1] for k in range(6)]
+    need("v", i_rowq)
+    perms = {}
+    perms[0] = perms[1] = ts(T.pmat[:, 128:256], T.rowq[:], pc, None, Op.is_equal)
+    need("v", c_i)
+    c_f = copy("v", T.pf[:, 0:6], T.pk[:, 0:6])
 
-    need("v", t_give)
-    c_gf = ts(T.gf[:], T.gi[:], 2.0, None, Op.mult)
-    need("v", c_gf)
-    c_d0 = ts(T.diag[:, 0:128], T.rowq[:], pc, T.gf[:, 0:1], Op.is_equal, Op.mult)
-    need("p", c_ones, c_d0)
-    p_b0 = done("p", mm(T.psm[:, 0:128], T.ones[:], T.diag[:, 0:128], True, True))
-    need("v", t_x)
-    c_xb = copy("v", T.xb[:], T.xi[:])
-    need("v", c_xb)
-    c_xt = done("v", g.vector.transpose(T.xt[:], T.xb[:]))
-    need("s", p_b0)
-    s_b0 = copy("s", T.giveb[:, 0:128], T.psm[:, 0:128])
-    xr = []
-    for q, k in (("s", 1), ("v", 0)):
-        need(q, c_xt, c_xl)
-        xr.append(copy(q, T.xr[:, 128 * k:128 * k + 128], T.xt[:, 0:256].indirect(T.xl[:, 8 * k:8 * k + 8])))
-    need("v", s_b0, c_v0)
-    g0 = {}
-    for idx in range(4):
-        for g2 in range(2):
-            k = 2 * idx + g2
-            g0[k] = ts(T.gm0[:, 128 * k:128 * k + 128], T.giveb[:, 0:128], -16.0 * g2, T.v0f[:, idx:idx + 1], Op.add, Op.is_equal)
-
-    others = [r for r in range(N) if r != rank]
-
-    def send(e, b, *tokens):
-        need("g", *tokens)
-        pools = [[], []]
-        for k, en in enumerate(topo.engines(core, cores[others[0]])):
-            pools[k % 2].append(en)
-        moves = []
-        for r in others:
-            dst = cores[r]
-            pool = pools[0 if topo.die(dst) != topo.die(core) else 1]
-            if len(pool) < 2:
-                pool = pools[0] if len(pools[0]) >= 2 else pools[1]
-            mask = 0
-            for _k in range(2):
-                mask |= 1 << pool.pop(0)
-            rid, pid = topo.addr(dst)[:2]
-            moves.append(RemoteDMATransfer(dst_ids=[DstId(rid=rid, pnc=pid)], dma_engine_mask=mask,
-                                           remote_sem=T.sem["arr%d%d" % (e, b)],
-                                           src=T["sb%d%d" % (e, b)][:, 32 * r:32 * r + 32],
-                                           dst=T["land%d%d" % (e, b)][:, 32 * rank:32 * rank + 32]))
-        g.remote_dma_fused(moves, local_sem=T.sem["loc"])
-        count["loc"] = count.get("loc", 0) + 2 * len(others)
-
-    def evac(q, e, b, c, tok):
-        need(q, tok)
-        return copy(q, T["sb%d%d" % (e, b)][:, c:256:2], T["psg%d" % (2 * b + c)][:, 0:128])
+    def codes(b):
+        need("v", t_x[b])
+        x1 = copy("v", T["xb%d" % b][:], T["xi%d" % b][:])
+        need("v", x1)
+        x2 = done("v", g.vector.transpose(T["xt%d" % b][:], T["xb%d" % b][:]))
+        need("p", x2, c_e0)
+        toks = []
+        for gb in range(2):
+            for z in range(2):
+                inst = mm(T["psg%d" % (2 * b + gb)][64 * z:64 * z + 64, 0:64], T["xt%d" % b][:, 64 * gb:64 * gb + 64],
+                          T.e0[:, 64 * z:64 * z + 64], True, True)
+            toks.append(done("p", inst))
+        return toks
 
     t_own = {}
 
-    def own(e, b, tokens):
-        need("v", *tokens)
-        t_own[(e, b)] = copy("v", T["land%d%d" % (e, b)][:, 32 * rank:32 * rank + 32], T["sb%d%d" % (e, b)][:, 32 * rank:32 * rank + 32])
-
-    need("p", *xr)
-    evs = []
-    for b in range(2):
-        p_g = []
+    def first(q, b, gb, tok):
+        need(q, tok)
         for c in range(2):
-            for z in range(2):
-                for g2 in range(2):
-                    k = 2 * (2 * c + z) + g2
-                    need("p", g0[k])
-                    inst = mm(T["psg%d" % (2 * b + c)][64 * z:64 * z + 64, 0:128], T.xr[:, 64 * (2 * g2 + b):64 * (2 * g2 + b) + 64],
-                              T.gm0[:, 128 * k:128 * k + 128], g2 == 0, g2 == 1)
-            p_g.append(done("p", inst))
-        ev = [evac("v", 0, b, 0, p_g[0]), evac("s", 0, b, 1, p_g[1])]
-        send(0, b, *ev)
-        evs.append(ev)
-    clear("g", 0, 3072)
+            at = 128 * rank + 64 * c + 32 * gb
+            t = copy(q, T["land0%d" % b][:, at:at + 32], T["psg%d" % (2 * b + gb)][:, 32 * c:32 * c + 32])
+        t_own.setdefault((0, b), []).append(t)
 
+    def evac(q, e, b, c, tok):
+        need(q, tok)
+        at = 128 * rank + 64 * c
+        t = copy(q, T["land%d%d" % (e, b)][:, at:at + 64], T["psg%d" % (2 * b + c)][:, 0:64])
+        t_own.setdefault((e, b), []).append(t)
+
+    def send_codes(e, b):
+        send("land%d%d" % (e, b), "arr%d%d" % (e, b), 128 * rank, 128 * rank + 128, *t_own[(e, b)])
+
+    def diag(e):
+        return done("s", g.scalar.activation(T.diag[:, 128 * e:128 * e + 128], T.pmat[:, 128:256], Copy, scale=T.wf[:, e:e + 1]))
+
+    p_x0 = codes(0)
+    p_x1 = codes(1)
     need("v", t_wire)
     c_wf = copy("v", T.wf[:], T.wi[:])
-    for e in range(1, 4):
-        c_d = ts(T.diag[:, 128 * e:128 * e + 128], T.rowq[:], pc, T.gf[:, e:e + 1], Op.is_equal, Op.mult)
-    need("v", i_row16, c_wf)
-    for l in range(4):
-        c_bm = ts(T.bmat[:, 16 * l:16 * l + 16], T.row16[:], T.p3f[:, 0:1], T.wf[:, l:l + 1], Op.is_equal, Op.mult)
-    need("p", c_am, c_bm, c_d)
-    p_b = done("p", mm(T.psm[:, 128:512], T.ones[:], T.diag[:, 128:512], True, True))
-    p_w = done("p", mm(T.psw[:, 0:64], T.amat[:], T.bmat[:], True, True))
-    need("s", p_b)
-    s_b = copy("s", T.giveb[:, 128:512], T.psm[:, 128:512])
-    for b in range(2):
-        own(0, b, evs[b])
-    need("v", p_w)
-    c_l = ts(T.lst[:], T.psw[:, 0:64], 2.0, T.hf[:, 0:1], Op.mult, Op.add)
-    gm = {}
+    first("s", 0, 0, p_x0[0])
+    first("v", 0, 1, p_x0[1])
+    send_codes(0, 0)
+    need("s", c_wf, perms[0])
+    c_d0 = diag(0)
+    need("p", c_ones, c_d0)
+    p_w0 = done("p", mm(T.psa0[:, 0:128], T.ones[:], T.diag[:, 0:128], True, True))
+    first("s", 1, 0, p_x1[0])
+    first("v", 1, 1, p_x1[1])
+    send_codes(0, 1)
+    for e in range(1, D):
+        c_d = diag(e)
+    need("p", c_d)
+    p_w = done("p", mm(T.psm[:, 128:512], T.ones[:], T.diag[:, 128:512], True, True))
+    i_rowa = iota(T.rowa[:], [[0, 16], [1, 8]], 0, 0)
+    i_rowu = iota(T.rowu[:], [[2, 8], [16, 8]], 0, 0)
+    i_rho3 = iota(T.rho3[:], [[2, 2], [4, 32], [1, 2]], 0, 0)
+    i_rho4 = iota(T.rho4[:], [[4, 32], [1, 2], [2, 2]], 0, 0)
+    i_k4 = iota(T.k4i[:], [[-4, 4]], 0, 1, True)
+    i_z = iota(T.zrow[:], [[16, 9], [-1000, 8], [0, 2]], 7000, 0)
+    clear("g", 6656, 8192)
 
-    def build_g(e):
-        odd = 1 if e == 2 else 0
-        need("v", s_b, c_cv)
-        for u in range(8):
-            gm[e] = ts(T["gm%d" % e][:, 128 * u:128 * u + 128], T.giveb[:, 128 * e:128 * e + 128], float(odd),
-                       T.cvf[:, 8 * odd + u:8 * odd + u + 1], Op.add, Op.is_equal)
+    x1 = ts(T.wqi[:], T.wi[:], 112, None, Op.bitwise_and)
+    need("v", i_rows)
+    c_sel = ts(T.selb[:], T.rows[:], pc, None, Op.is_equal)
+    need("v", p_w0)
+    c_oh0 = ts(T.oh[:, 0:128], T.psa0[:, 0:128], pc, None, Op.is_equal)
+    need("v", x1, c_f, i_row16)
+    c_wq = ts(T.wqf[:], T.wqi[:], 8.0, None, Op.mult)
+    c_mk = ts(T.mask[:], T.rowm[:], pq, None, Op.is_equal)
+    ts(T.hf[:], h8, 8.0, None, Op.mult)
+    need("v", c_wq)
 
-    build_g(1)
-    clear("s", 3072, 4096)
+    def ranks(a, b):
+        for e in range(a, b):
+            t = ts(T.bmq[:, 16 * e:16 * e + 16], T.row16[:], p3, T.wqf[:, e:e + 1], Op.is_equal, Op.mult)
+        return t
 
-    perms = {0: c_perm1, 1: c_perm1}
-    y_banks = [T.psm, T.psw, T.psg0, T.psg1]
+    c_bq = {0: ranks(0, 1)}
+    need("v", t_give, ("arrg", arrive))
+    c_gl = copy("v", T.glb[:], T.gl[:])
+    need("p", c_sel, c_gl)
+    p_c = done("p", mm(T.psw[:, 64:96], T.selb[:], T.glb[:], True, True))
+    need("v", i_rowa)
+    c_am = ts(T.amat[:], T.rowa[:], p7, None, Op.is_equal)
+    need("v", p_c, c_mk)
+    c_mg = done("v", g.vector.tensor_tensor(T.gmk[:], T.psw[:, 64:96], T.mask[:], Op.mult))
+    need("v", c_mg)
+
+    def units_of(e):
+        return done("v", g.vector.tensor_reduce(T.cmpb[:, e:e + 1], T.gmk[:, e:32:4], AxisListType.X, Op.max))
+
+    c_c = units_of(0)
+    need("p", c_c, c_oh0)
+    p_n = {0: done("p", mm(T.psa0[:, 128:129], T.oh[:, 0:128], T.cmpb[:, 0:1], True, True))}
+    t_l = {}
+    c_bn = {}
+    c_un = {1: units_of(1)}
+
+    def spread(e):
+        need("v", p_n[e])
+        src = T.psm[:, e:e + 1] if e else T.psa0[:, 128:129]
+        c_bn[e] = ts(T.bmn[:, 16 * e:16 * e + 16], T.row16[:], p3, src, Op.is_equal, Op.mult)
+
+    def lists(a, b):
+        need("p", c_am, c_bq[b - 1], c_bn[b - 1])
+        mm(T.psw[:, 16 * a:16 * b], T.amat[:], T.bmq[:, 16 * a:16 * b], True, False)
+        return done("p", mm(T.psw[:, 16 * a:16 * b], T.amat[:], T.bmn[:, 16 * a:16 * b], False, True))
+
+    def put_lists(a, b, tok):
+        need("v", tok)
+        t = ts(T.lst[:, 16 * a:16 * b], T.psw[:, 16 * a:16 * b], T.hf[:, 0:1], None, Op.add)
+        for e in range(a, b):
+            t_l[e] = t
+
+    spread(0)
+    perms["l0"] = lists(0, 1)
+    perms[0] = perms[1] = ts(T.pmat[:, 0:128], T.rowq[:], pc, 64.0, Op.is_equal, Op.mult)
+    c_un[2] = units_of(2)
+    put_lists(0, 1, perms["l0"])
+    for k in range(6, 9):
+        clear("s", 512 * k, 512 * k + 512)
+
+    units = {}
+    y_banks = [[T.psm, T.psw, T.psg0, T.psg1], [T.psg2, T.psg3, T.psa0, T.psa1]]
+    fin = {0: [], 1: []}
+    t_y = {}
+
+    def hot(a, b):
+        need("v", p_w)
+        t = ts(T.oh[:, 128 * a:128 * b], T.psm[:, 128 * a:128 * b], pc, None, Op.is_equal)
+        for j in range(a, b):
+            need("p", t, c_un[j])
+            inst = mm(T.psm[:, j:j + 1], T.oh[:, 128 * j:128 * j + 128], T.cmpb[:, j:j + 1], True, True)
+        t = done("p", inst)
+        for j in range(a, b):
+            p_n[j] = t
+
+    def spare(e):
+        if e == 0:
+            hot(1, 2)
+            need("v", i_rowu)
+            units[1] = units[3] = (T.ev, ts(T.ev[:], T.rowu[:], pc, None, Op.is_equal))
+        elif e == 1:
+            spread(2)
+            spread(3)
+            perms["l2"] = lists(2, D)
+            units[2] = (T.od, ts(T.od[:], T.rowu[:], 1.0, pc, Op.add, Op.is_equal))
+        elif e == 2:
+            need("v", i_rho4)
+            ts(T.pmat[:, 512:640], T.rho4[:], pc, 64.0, Op.is_equal, Op.mult)
+            perms[3] = ts(T.pmat[:, 640:768], T.rho4[:], pc, None, Op.is_equal)
+            perms["u2"] = ts(T.u2f[:], u4, 1024.0, None, Op.mult)
+
+    def between(e):
+        if e == 0:
+            put_lists(1, 2, perms["l1"])
+            c_un[3] = units_of(3)
+            hot(2, D)
+            c_bq[D - 1] = ranks(2, D)
+            clear("g", 5632, 6656)
+        elif e == 1:
+            put_lists(2, D, perms["l2"])
+            need("v", i_rho3, i_k4)
+            ts(T.pmat[:, 256:384], T.rho3[:], pc, 64.0, Op.is_equal, Op.mult)
+            perms[2] = ts(T.pmat[:, 384:512], T.rho3[:], pc, None, Op.is_equal)
+            perms["k4"] = ts(T.k4j[:], T.k4i[:], 13, None, Op.bitwise_and)
+            clear("g", 4608, 5632)
+        elif e == 2:
+            need("v", i_z, perms["k4"])
+            c1 = ts(T.k4f[:], T.k4j[:], -1000.0, g16, Op.mult, Op.add)
+            need("v", c1)
+            for v in range(4):
+                perms["base"] = ts(T.base[:, 144 * v:144 * v + 144], T.zrow[:], T.k4f[:, v:v + 1], None, Op.is_equal)
 
     for e in range(D):
         last = e == D - 1
@@ -247,63 +328,83 @@ def rank_program(g, core, T, topo):
         pk = (0, 0, 256, 512)[e]
         sel, pa, off = {}, {}, {}
         tok = {}
-        pieces = {}
-        for b in range(2):
-            pieces[b], at = [], 0
-            for n in ((2, 1, 1) if last or b == 0 else (2, 2)):
-                pieces[b].append((at, at + n, at + 2 * n))
-                at += 2 * n
+        pieces = {0: [(0, 30, 64), (64, 80, 96), (96, 112, 128)],
+                  1: [(0, 16, 32), (32, 48, 64), (64, 80, 96), (96, 112, 128)] if last else [(0, 16, 32), (32, 48, 64), (64, 96, 128)]}
 
         def pick(q, b):
             i = 0 if q == "v" else 1
-            need(q, ("arr%d%d" % (e, b), 2 * len(others)), t_own[(e, b)], c_l)
-            sel[(q, b)] = copy(q, T["sel%d" % (2 * b + i)][:], T["land%d%d" % (e, b)][:, 0:256].indirect(T.lst[:, 16 * e + 8 * i:16 * e + 8 * i + 8]))
+            need(q, ("arr%d%d" % (e, b), arrive), t_l[e], *t_own[(e, b)])
+            sel[(q, b)] = copy(q, T["sel%d" % (2 * b + i)][:], T["land%d%d" % (e, b)][:, 0:1024].indirect(T.lst[:, 16 * e + 8 * i:16 * e + 8 * i + 8]))
+
+        def halves(b):
+            return [(T.psa0, 0, 64), (T.psg2, 64, 128)] if b == 0 else [(T.psa1, 0, 128)]
 
         def turn(b):
-            for i, q in enumerate("vs"):
-                need("p", perms[e], sel[(q, b)])
-                inst = mm(T["psa%d" % b][:, 0:128], T["sel%d" % (2 * b + i)][:], T.pmat[:, pk + 128 * i:pk + 128 * i + 128], i == 0, i == 1)
-            pa[b] = done("p", inst)
+            need("p", perms[e], *t_own[(e, 1)])
+            pa[b] = []
+            for bank, lo, hi in halves(b):
+                for i, q in enumerate("vs"):
+                    need("p", sel[(q, b)])
+                    at = pk + 128 * i
+                    inst = mm(bank[:, lo:hi], T["sel%d" % (2 * b + i)][:], T.pmat[:, at + lo:at + hi], i == 0, i == 1)
+                pa[b].append(done("p", inst))
 
         def cast(b):
-            need("v", pa[b])
-            o, i = T["offs%d" % b][:], T["psa%d" % b][:, 0:128]
-            off[b] = ts(o, i, T.u2f[:, 0:1], None, Op.add) if last else copy("v", o, i)
+            off[b] = []
+            for t, (bank, lo, hi) in zip(pa[b], halves(b)):
+                need("v", t)
+                o, i = T["offs%d" % b][:, lo:hi], bank[:, lo:hi]
+                off[b].append(ts(o, i, T.u2f[:, 0:1], None, Op.add) if last else copy("v", o, i))
 
         def look(q, b, j):
             x, y, z = pieces[b][j]
             lo, hi = (x, y) if q == "v" else (y, z)
-            need(q, t_tab[e], off[b])
-            win = tab[:, 0:8192 if last else 4096].indirect(T["offs%d" % b][:, 16 * lo:16 * hi])
-            tok[(q, b, j)] = copy(q, T["rr%d" % b][:, 256 * lo:256 * hi], win)
+            need(q, t_tab[e], off[b][0 if j == 0 else -1])
+            win = tab[:, 0:8192 if last else 4096].indirect(T["offs%d" % b][:, lo:hi])
+            tok[(q, b, j)] = copy(q, T["rr%d" % b][:, 16 * lo:16 * hi], win)
 
         def give(b, c):
-            hit = [k for k in range(len(pieces[b])) if pieces[b][k][2] == 4 * c + 4][0]
-            need("p", tok[("v", b, hit)], tok[("s", b, hit)], gm[e + 1])
+            hit = [k for k in range(len(pieces[b])) if pieces[b][k][2] == 64 * c + 64][0]
+            mat, c_mat = units[e + 1]
+            need("p", tok[("v", b, hit)], tok[("s", b, hit)], c_mat)
             for u in range(8):
-                inst = mm(T["psg%d" % (2 * b + c)][:, 0:128], T["rr%d" % b][:, 1024 * c + u:1024 * c + 1024:8],
-                          T["gm%d" % (e + 1)][:, 128 * u:128 * u + 128], u == 0, u == 7)
+                inst = mm(T["psg%d" % (2 * b + c)][:, u:64:8], T["rr%d" % b][:, 1024 * c + u:1024 * c + 1024:8],
+                          mat[:, 8 * u:8 * u + 8], True, True)
             return done("p", inst)
 
         p_y = {}
 
         def place(b, j):
             x, y, z = pieces[b][j]
-            for k in range(x, z):
-                need("p", tok[("v" if k < y else "s", b, j)])
-                s = 8 * b + k
-                for v in range(4):
-                    at = 144 * v + 15 - s
-                    inst = mm(y_banks[v][:, 0:64], T.base[:, at:at + 128], T["rr%d" % b][:, 256 * k + v:256 * k + 256:4], s == 0, s == 15)
-                    if s == 15:
-                        p_y[v] = done("p", inst)
+            blocks = [(k, v) for k in range(x // 16, z // 16) for v in range(4)]
+            if z == 128:
+                blocks = [(k, v) for v in range(4) for k in range(x // 16, z // 16)]
+            for k, v in blocks:
+                if 16 * k < y:
+                    need("p", tok[("v", b, j)])
+                if 16 * k + 16 > y:
+                    need("p", tok[("s", b, j)])
+                at = 144 * v + 14 - 2 * k
+                inst = mm(y_banks[b][v][:, 0:64], T.base[:, at:at + 128], T["rr%d" % b][:, 256 * k + v:256 * k + 256:4], k == 0, k == 7)
+                if k == 7:
+                    p_y[(b, v)] = done("p", inst)
+
+        def out(q, b, v):
+            need(q, p_y[(b, v)])
+            fin[b].append(copy(q, T["ysb%d" % b][:, v:256:4], y_banks[b][v][:, 0:64]))
+
+        def store(b, queue):
+            for k in range(2):
+                need(queue[k], *fin[b])
+                t_y[k] = dma(queue[k], T.y[k::2, 128 * b:128 * b + 128], T["ysb%d" % b][k::2, 128 * k:128 * k + 128], "dy")
 
         for q in "vs":
             pick(q, 0)
         turn(0)
+        spare(e)
         if last:
-            need("v", c_u2)
-            need("p", c_base)
+            need("v", perms["u2"])
+            need("p", perms["base"])
         cast(0)
         for k in range(3):
             if k == 2:
@@ -322,20 +423,26 @@ def rank_program(g, core, T, topo):
             turn(1)
             p0.append(give(0, 1))
             cast(1)
-            ev0 = [evac("v", e + 1, 0, 0, p0[0])]
+            evac("v", e + 1, 0, 0, p0[0])
+            if e == 0:
+                c_bq[1] = ranks(1, 2)
+                spread(1)
+                perms["l1"] = lists(1, 2)
         for k in range(len(pieces[1])):
             for q in "vs":
                 look(q, 1, k)
             if k == 0 and not last:
-                ev0.append(evac("s", e + 1, 0, 1, p0[1]))
-                send(e + 1, 0, *ev0)
-        need("y", ("arr%d1" % e, 2 * len(others)))
+                evac("s", e + 1, 0, 1, p0[1])
+                send_codes(e + 1, 0)
+            if k == 1 and last:
+                for v, q in enumerate("vsvs"):
+                    out(q, 0, v)
+                store(0, "yy")
+        need("y", ("arr%d1" % e, arrive))
         if e == 0:
             dma("y", T.tab1[0::2, :], T.tb[:, 2 * W:3 * W], "dt1")
         elif e == 1:
             t_tab[2] = dma("y", T.tab1[1::2, :], T.tb[:, 2 * W:3 * W], "dt1")
-            need("y", *zero)
-            zero.append(dma("y", T.tab3[:, 6144:8192], T.tab3[:, 0:2048], "dz"))
         elif e == 2:
             need("y", *zero)
             dma("y", T.tab3[0::4, 0:4096], T.tb[:, 3 * W:3 * W + W // 2], "dt3")
@@ -343,38 +450,14 @@ def rank_program(g, core, T, topo):
         if last:
             for k in range(len(pieces[1])):
                 place(1, k)
+            for v, q in enumerate("vsvs"):
+                out(q, 1, v)
+            store(1, "ys")
+            need("y", *t_y.values())
             break
         p1 = [give(1, c) for c in range(2)]
-        own(e + 1, 0, ev0)
-        ev1 = [evac("v", e + 1, 1, 0, p1[0]), evac("s", e + 1, 1, 1, p1[1])]
-        send(e + 1, 1, *ev1)
-        if e == 0:
-            clear("g", 4096, 6144)
-            build_g(2)
-        elif e == 1:
-            build_g(3)
-            need("v", i_rho3, i_rho4)
-            for k, rho in ((256, T.rho3), (512, T.rho4)):
-                ts(T.pmat[:, k:k + 128], rho[:], pc, 64.0, Op.is_equal, Op.mult)
-                perms[2] = perms[3] = ts(T.pmat[:, k + 128:k + 256], rho[:], pc, None, Op.is_equal)
-        else:
-            need("v", i_k4, i_z)
-            ts(T.k4j[:], T.k4i[:], 13, None, Op.bitwise_and)
-            bits("g16", 0, 112)
-            x1 = bits("u2", 2, 1)
-            need("v", x1)
-            x2 = copy("v", T.g16f[:], T.g16i[:])
-            c_u2 = ts(T.u2f[:], T.u2i[:], 4096.0, None, Op.mult)
-            need("v", x2)
-            x3 = ts(T.k4f[:], T.k4j[:], -1000.0, T.g16f[:, 0:1], Op.mult, Op.add)
-            need("v", x3)
-            for v in range(4):
-                c_base = ts(T.base[:, 144 * v:144 * v + 144], T.zrow[:], T.k4f[:, v:v + 1], None, Op.is_equal)
-        own(e + 1, 1, ev1)
-    fin = []
-    for v, q in enumerate("vsvs"):
-        need(q, p_y[v])
-        fin.append(copy(q, T.ysb[:, v:256:4], y_banks[v][:, 0:64]))
-    need("y", *fin)
-    need("y", dma("y", T.y[:, :], T.ysb[:], "dy"))
+        evac("v", e + 1, 1, 0, p1[0])
+        evac("s", e + 1, 1, 1, p1[1])
+        send_codes(e + 1, 1)
+        between(e)
     need("g", *[(n, count[n]) for n in ("qv", "qs", "qp", "qg", "loc")])

from concourse.bass import DstId, RemoteDMATransfer
from concourse.mybir import dt, AluOpType, AxisListType, ActivationFunctionType

BF, F32, I32, U16 = "bfloat16", "float32", "int32", "uint16"
D = 4

SCRATCH = {}
for _t, _names in ((BF, "xb0 128 xb1 128 xt0 128 xt1 128 diag 512 oh 512 glb 32 gmk 32 cmpb 4 sel0 128 sel1 128 sel2 128 sel3 128 "
                        "rr0 2048 rr1 2048 tab0 4096 tab1 4096 tab3 8192 rowq 128 rowe 128 rowa 128 row16 16 rowu 64 rows 128 "
                        "rowm 32 mask 32 rho3 128 rho4 128 zrow 144 ones 128 amat 128 bmq 64 bmn 64 base 576 pmat 768 e0 128 "
                        "ev 64 od 64 selb 128"),
                   (F32, "wf 4 wqf 4 ysb0 256 ysb1 256 pcol 1 k4f 4 pf 8 hf 1 u2f 1"),
                   (I32, "xi0 128 xi1 128 gl 32 wi 4 wqi 4 pint 1 k4i 4 k4j 4 pk 8"),
                   (U16, "offs0 128 offs1 128 lst 64")):
    _w = _names.split()
    for _k in range(0, len(_w), 2):
        SCRATCH[_w[_k]] = ("sbuf", [128, int(_w[_k + 1])], _t)
for _e in range(4):
    for _b in range(2):
        SCRATCH["land%d%d" % (_e, _b)] = ("sbuf", [128, 1024], BF)
for _n in ("psg0", "psg1", "psg2", "psg3", "psa0", "psa1", "psm", "psw"):
    SCRATCH[_n] = ("psum", [128, 512], F32)

SEMAPHORES = ["qv", "qs", "qp", "qg", "loc", "dgive", "dwire", "dx0", "dx1", "dt0", "dt1", "dt3", "dy", "arrg"]
SEMAPHORES += ["arr%d%d" % (_e, _b) for _e in range(4) for _b in range(2)]


def rank_program(g, core, T, topo):
    rank = T.rank_of(core)
    if rank is None:
        return
    cores = T.cores
    N = len(cores)
    Op = AluOpType
    Copy = ActivationFunctionType.Copy
    queues = {"v": g.vector, "s": g.scalar, "p": g.tensor, "g": g, "y": g.sync}
    count = {}
    seen = {}

    def need(q, *tokens):
        want = {}
        for name, val in tokens:
            want[name] = max(val, want.get(name, 0))
        for name in sorted(want):
            if seen.get((q, name), 0) < want[name]:
                queues[q].wait_ge(T.sem[name], want[name])
                seen[(q, name)] = want[name]

    def done(q, inst):
        name = "q" + q
        count[name] = count.get(name, 0) + 1
        inst.then_inc(T.sem[name], 1)
        return (name, count[name])

    def dma(q, out, in_, name):
        count[name] = count.get(name, 0) + 16
        queues[q].dma_start(out, in_).then_inc(T.sem[name], 16)
        return (name, count[name])

    def ts(out, in0, s1, s2, op0, op1=None):
        if op1 is None:
            return done("v", g.vector.tensor_scalar(out, in0, s1, s2, op0))
        return done("v", g.vector.tensor_scalar(out, in0, s1, s2, op0, op1))

    def copy(q, out, in_):
        if q == "v":
            return done("v", g.vector.tensor_copy(out, in_))
        return done("s", g.scalar.activation(out, in_, Copy))

    def iota(out, pattern, base, mult, whole=False):
        if whole:
            return done("g", g.iota(out, pattern, base, mult))
        return done("g", g.iota(out, pattern, base, mult, allow_small_or_imprecise_dtypes=True))

    def mm(out, lhsT, rhs, start, stop):
        return g.tensor.matmul(out, lhsT, rhs, start, stop)

    others = [cores[(rank + k) % N] for k in range(1, N)]
    engines = topo.mask(core, others[0])
    for dst in others:
        engines &= topo.mask(core, dst)
    n_eng = len([k for k in topo.engines(core, others[0]) if engines >> k & 1])
    arrive = n_eng * len(others)

    def send(name, arr, lo, hi, *tokens):
        need("g", *tokens)
        ids = [DstId(rid=topo.addr(dst)[0], pnc=topo.addr(dst)[1]) for dst in others]
        part = T[name][:, lo:hi]
        g.remote_dma_fused([RemoteDMATransfer(dst_ids=ids, dma_engine_mask=engines, remote_sem=T.sem[arr],
                                              srcs=[part], dsts=[part] * len(others))], local_sem=T.sem["loc"])
        count["loc"] = count.get("loc", 0) + n_eng

    t_x = {}

    def load_x(q, b, gb):
        for z in range(2):
            at = 128 * b + 64 * z
            t_x[b] = dma(q, T["xi%d" % b][z::2, 64 * gb:64 * gb + 64], T.x[64 * gb:64 * gb + 64, at:at + 64], "dx%d" % b)

    t_give = dma("y", T.gl[:, 4 * rank:4 * rank + 4], T.give[:, :], "dgive")
    load_x("s", 0, 0)
    load_x("y", 0, 1)
    load_x("s", 1, 0)
    load_x("y", 1, 1)
    t_wire = dma("y", T.wi[:], T.wires[:, :], "dwire")
    W = 8 * 4096
    t_tab = {}
    dma("y", T.tab0[0::2, :], T.tb[:, 0:W], "dt0")
    t_tab[0] = t_tab[1] = dma("y", T.tab0[1::2, :], T.tb[:, W:2 * W], "dt0")

    i_pcol = iota(T.pcol[:], [[0, 1]], 0, 1)
    i_pint = iota(T.pint[:], [[0, 1]], 0, 1, True)
    i_rowe = iota(T.rowe[:], [[8, 4], [32, 4], [1, 8]], 0, 0)
    i_rowq = iota(T.rowq[:], [[1, 128]], 0, 0)
    i_rows = iota(T.rows[:], [[0, 8], [1, 16]], 16 * rank, 0)
    i_rowm = iota(T.rowm[:], [[1, 8], [0, 4]], 0, 0)
    i_row16 = iota(T.row16[:], [[1, 2], [2, 8]], 0, 0)
    send("gl", "arrg", 4 * rank, 4 * rank + 4, t_give)

    pc = T.pcol[:, 0:1]
    zero = [done("v", g.vector.memset(T.tab3[:, 0:512], 0.0)), done("v", g.vector.memset(T.tab3[:, 512:1536], 0.0))]

    def clear(q, a, b):
        part = T.tab3[:, a:b]
        if q == "g":
            zero.append(iota(part, [[0, b - a]], 0, 0))
        else:
            need("s", zero[0])
            zero.append(copy("s", part, T.tab3[:, 0:b - a]))

    for k in range(3, 6):
        clear("s", 512 * k, 512 * k + 512)
    c_ones = done("v", g.vector.memset(T.ones[:], 1.0))
    need("v", i_pint, i_rowe)
    c_e0 = ts(T.e0[:], T.rowe[:], pc, None, Op.is_equal)

    def bits(k, shift, mask):
        if shift:
            return ts(T.pk[:, k:k + 1], T.pint[:], shift, mask, Op.arith_shift_right, Op.bitwise_and)
        return ts(T.pk[:, k:k + 1], T.pint[:], mask, None, Op.bitwise_and)

    for k, (sh, mk) in enumerate(((0, 7), (3, 15), (4, 7), (0, 8), (0, 4), (0, 112))):
        c_i = bits(k, sh, mk)
    p7, p3, pq, h8, u4, g16 = [T.pf[:, k:k + 1] for k in range(6)]
    need("v", i_rowq)
    perms = {}
    perms[0] = perms[1] = ts(T.pmat[:, 128:256], T.rowq[:], pc, None, Op.is_equal)
    need("v", c_i)
    c_f = copy("v", T.pf[:, 0:6], T.pk[:, 0:6])

    def codes(b):
        need("v", t_x[b])
        x1 = copy("v", T["xb%d" % b][:], T["xi%d" % b][:])
        need("v", x1)
        x2 = done("v", g.vector.transpose(T["xt%d" % b][:], T["xb%d" % b][:]))
        need("p", x2, c_e0)
        toks = []
        for gb in range(2):
            for z in range(2):
                inst = mm(T["psg%d" % (2 * b + gb)][64 * z:64 * z + 64, 0:64], T["xt%d" % b][:, 64 * gb:64 * gb + 64],
                          T.e0[:, 64 * z:64 * z + 64], True, True)
            toks.append(done("p", inst))
        return toks

    t_own = {}

    def first(q, b, gb, tok):
        need(q, tok)
        for c in range(2):
            at = 128 * rank + 64 * c + 32 * gb
            t = copy(q, T["land0%d" % b][:, at:at + 32], T["psg%d" % (2 * b + gb)][:, 32 * c:32 * c + 32])
        t_own.setdefault((0, b), []).append(t)

    def evac(q, e, b, c, tok):
        need(q, tok)
        at = 128 * rank + 64 * c
        t = copy(q, T["land%d%d" % (e, b)][:, at:at + 64], T["psg%d" % (2 * b + c)][:, 0:64])
        t_own.setdefault((e, b), []).append(t)

    def send_codes(e, b):
        send("land%d%d" % (e, b), "arr%d%d" % (e, b), 128 * rank, 128 * rank + 128, *t_own[(e, b)])

    def diag(e):
        return done("s", g.scalar.activation(T.diag[:, 128 * e:128 * e + 128], T.pmat[:, 128:256], Copy, scale=T.wf[:, e:e + 1]))

    p_x0 = codes(0)
    p_x1 = codes(1)
    need("v", t_wire)
    c_wf = copy("v", T.wf[:], T.wi[:])
    first("s", 0, 0, p_x0[0])
    first("v", 0, 1, p_x0[1])
    send_codes(0, 0)
    need("s", c_wf, perms[0])
    c_d0 = diag(0)
    need("p", c_ones, c_d0)
    p_w0 = done("p", mm(T.psa0[:, 0:128], T.ones[:], T.diag[:, 0:128], True, True))
    first("s", 1, 0, p_x1[0])
    first("v", 1, 1, p_x1[1])
    send_codes(0, 1)
    for e in range(1, D):
        c_d = diag(e)
    need("p", c_d)
    p_w = done("p", mm(T.psm[:, 128:512], T.ones[:], T.diag[:, 128:512], True, True))
    i_rowa = iota(T.rowa[:], [[0, 16], [1, 8]], 0, 0)
    i_rowu = iota(T.rowu[:], [[2, 8], [16, 8]], 0, 0)
    i_rho3 = iota(T.rho3[:], [[2, 2], [4, 32], [1, 2]], 0, 0)
    i_rho4 = iota(T.rho4[:], [[4, 32], [1, 2], [2, 2]], 0, 0)
    i_k4 = iota(T.k4i[:], [[-4, 4]], 0, 1, True)
    i_z = iota(T.zrow[:], [[16, 9], [-1000, 8], [0, 2]], 7000, 0)
    clear("g", 6656, 8192)

    x1 = ts(T.wqi[:], T.wi[:], 112, None, Op.bitwise_and)
    need("v", i_rows)
    c_sel = ts(T.selb[:], T.rows[:], pc, None, Op.is_equal)
    need("v", p_w0)
    c_oh0 = ts(T.oh[:, 0:128], T.psa0[:, 0:128], pc, None, Op.is_equal)
    need("v", x1, c_f, i_row16)
    c_wq = ts(T.wqf[:], T.wqi[:], 8.0, None, Op.mult)
    c_mk = ts(T.mask[:], T.rowm[:], pq, None, Op.is_equal)
    ts(T.hf[:], h8, 8.0, None, Op.mult)
    need("v", c_wq)

    def ranks(a, b):
        for e in range(a, b):
            t = ts(T.bmq[:, 16 * e:16 * e + 16], T.row16[:], p3, T.wqf[:, e:e + 1], Op.is_equal, Op.mult)
        return t

    c_bq = {0: ranks(0, 1)}
    need("v", t_give, ("arrg", arrive))
    c_gl = copy("v", T.glb[:], T.gl[:])
    need("p", c_sel, c_gl)
    p_c = done("p", mm(T.psw[:, 64:96], T.selb[:], T.glb[:], True, True))
    need("v", i_rowa)
    c_am = ts(T.amat[:], T.rowa[:], p7, None, Op.is_equal)
    need("v", p_c, c_mk)
    c_mg = done("v", g.vector.tensor_tensor(T.gmk[:], T.psw[:, 64:96], T.mask[:], Op.mult))
    need("v", c_mg)

    def units_of(e):
        return done("v", g.vector.tensor_reduce(T.cmpb[:, e:e + 1], T.gmk[:, e:32:4], AxisListType.X, Op.max))

    c_c = units_of(0)
    need("p", c_c, c_oh0)
    p_n = {0: done("p", mm(T.psa0[:, 128:129], T.oh[:, 0:128], T.cmpb[:, 0:1], True, True))}
    t_l = {}
    c_bn = {}
    c_un = {1: units_of(1)}

    def spread(e):
        need("v", p_n[e])
        src = T.psm[:, e:e + 1] if e else T.psa0[:, 128:129]
        c_bn[e] = ts(T.bmn[:, 16 * e:16 * e + 16], T.row16[:], p3, src, Op.is_equal, Op.mult)

    def lists(a, b):
        need("p", c_am, c_bq[b - 1], c_bn[b - 1])
        mm(T.psw[:, 16 * a:16 * b], T.amat[:], T.bmq[:, 16 * a:16 * b], True, False)
        return done("p", mm(T.psw[:, 16 * a:16 * b], T.amat[:], T.bmn[:, 16 * a:16 * b], False, True))

    def put_lists(a, b, tok):
        need("v", tok)
        t = ts(T.lst[:, 16 * a:16 * b], T.psw[:, 16 * a:16 * b], T.hf[:, 0:1], None, Op.add)
        for e in range(a, b):
            t_l[e] = t

    spread(0)
    perms["l0"] = lists(0, 1)
    perms[0] = perms[1] = ts(T.pmat[:, 0:128], T.rowq[:], pc, 64.0, Op.is_equal, Op.mult)
    c_un[2] = units_of(2)
    put_lists(0, 1, perms["l0"])
    for k in range(6, 9):
        clear("s", 512 * k, 512 * k + 512)

    units = {}
    y_banks = [[T.psm, T.psw, T.psg0, T.psg1], [T.psg2, T.psg3, T.psa0, T.psa1]]
    fin = {0: [], 1: []}
    t_y = {}

    def hot(a, b):
        need("v", p_w)
        t = ts(T.oh[:, 128 * a:128 * b], T.psm[:, 128 * a:128 * b], pc, None, Op.is_equal)
        for j in range(a, b):
            need("p", t, c_un[j])
            inst = mm(T.psm[:, j:j + 1], T.oh[:, 128 * j:128 * j + 128], T.cmpb[:, j:j + 1], True, True)
        t = done("p", inst)
        for j in range(a, b):
            p_n[j] = t

    def spare(e):
        if e == 0:
            hot(1, 2)
            need("v", i_rowu)
            units[1] = units[3] = (T.ev, ts(T.ev[:], T.rowu[:], pc, None, Op.is_equal))
        elif e == 1:
            spread(2)
            spread(3)
            perms["l2"] = lists(2, D)
            units[2] = (T.od, ts(T.od[:], T.rowu[:], 1.0, pc, Op.add, Op.is_equal))
        elif e == 2:
            need("v", i_rho4)
            ts(T.pmat[:, 512:640], T.rho4[:], pc, 64.0, Op.is_equal, Op.mult)
            perms[3] = ts(T.pmat[:, 640:768], T.rho4[:], pc, None, Op.is_equal)
            perms["u2"] = ts(T.u2f[:], u4, 1024.0, None, Op.mult)

    def between(e):
        if e == 0:
            put_lists(1, 2, perms["l1"])
            c_un[3] = units_of(3)
            hot(2, D)
            c_bq[D - 1] = ranks(2, D)
            clear("g", 5632, 6656)
        elif e == 1:
            put_lists(2, D, perms["l2"])
            need("v", i_rho3, i_k4)
            ts(T.pmat[:, 256:384], T.rho3[:], pc, 64.0, Op.is_equal, Op.mult)
            perms[2] = ts(T.pmat[:, 384:512], T.rho3[:], pc, None, Op.is_equal)
            perms["k4"] = ts(T.k4j[:], T.k4i[:], 13, None, Op.bitwise_and)
            clear("g", 4608, 5632)
        elif e == 2:
            need("v", i_z, perms["k4"])
            c1 = ts(T.k4f[:], T.k4j[:], -1000.0, g16, Op.mult, Op.add)
            need("v", c1)
            for v in range(4):
                perms["base"] = ts(T.base[:, 144 * v:144 * v + 144], T.zrow[:], T.k4f[:, v:v + 1], None, Op.is_equal)

    for e in range(D):
        last = e == D - 1
        tab = T["tab%d" % (0, 0, 1, 3)[e]]
        pk = (0, 0, 256, 512)[e]
        sel, pa, off = {}, {}, {}
        tok = {}
        pieces = {0: [(0, 30, 64), (64, 80, 96), (96, 112, 128)],
                  1: [(0, 16, 32), (32, 48, 64), (64, 80, 96), (96, 112, 128)] if last else [(0, 16, 32), (32, 48, 64), (64, 96, 128)]}

        def pick(q, b):
            i = 0 if q == "v" else 1
            need(q, ("arr%d%d" % (e, b), arrive), t_l[e], *t_own[(e, b)])
            sel[(q, b)] = copy(q, T["sel%d" % (2 * b + i)][:], T["land%d%d" % (e, b)][:, 0:1024].indirect(T.lst[:, 16 * e + 8 * i:16 * e + 8 * i + 8]))

        def halves(b):
            return [(T.psa0, 0, 64), (T.psg2, 64, 128)] if b == 0 else [(T.psa1, 0, 128)]

        def turn(b):
            need("p", perms[e], *t_own[(e, 1)])
            pa[b] = []
            for bank, lo, hi in halves(b):
                for i, q in enumerate("vs"):
                    need("p", sel[(q, b)])
                    at = pk + 128 * i
                    inst = mm(bank[:, lo:hi], T["sel%d" % (2 * b + i)][:], T.pmat[:, at + lo:at + hi], i == 0, i == 1)
                pa[b].append(done("p", inst))

        def cast(b):
            off[b] = []
            for t, (bank, lo, hi) in zip(pa[b], halves(b)):
                need("v", t)
                o, i = T["offs%d" % b][:, lo:hi], bank[:, lo:hi]
                off[b].append(ts(o, i, T.u2f[:, 0:1], None, Op.add) if last else copy("v", o, i))

        def look(q, b, j):
            x, y, z = pieces[b][j]
            lo, hi = (x, y) if q == "v" else (y, z)
            need(q, t_tab[e], off[b][0 if j == 0 else -1])
            win = tab[:, 0:8192 if last else 4096].indirect(T["offs%d" % b][:, lo:hi])
            tok[(q, b, j)] = copy(q, T["rr%d" % b][:, 16 * lo:16 * hi], win)

        def give(b, c):
            hit = [k for k in range(len(pieces[b])) if pieces[b][k][2] == 64 * c + 64][0]
            mat, c_mat = units[e + 1]
            need("p", tok[("v", b, hit)], tok[("s", b, hit)], c_mat)
            for u in range(8):
                inst = mm(T["psg%d" % (2 * b + c)][:, u:64:8], T["rr%d" % b][:, 1024 * c + u:1024 * c + 1024:8],
                          mat[:, 8 * u:8 * u + 8], True, True)
            return done("p", inst)

        p_y = {}

        def place(b, j):
            x, y, z = pieces[b][j]
            blocks = [(k, v) for k in range(x // 16, z // 16) for v in range(4)]
            if z == 128:
                blocks = [(k, v) for v in range(4) for k in range(x // 16, z // 16)]
            for k, v in blocks:
                if 16 * k < y:
                    need("p", tok[("v", b, j)])
                if 16 * k + 16 > y:
                    need("p", tok[("s", b, j)])
                at = 144 * v + 14 - 2 * k
                inst = mm(y_banks[b][v][:, 0:64], T.base[:, at:at + 128], T["rr%d" % b][:, 256 * k + v:256 * k + 256:4], k == 0, k == 7)
                if k == 7:
                    p_y[(b, v)] = done("p", inst)

        def out(q, b, v):
            need(q, p_y[(b, v)])
            fin[b].append(copy(q, T["ysb%d" % b][:, v:256:4], y_banks[b][v][:, 0:64]))

        def store(b, queue):
            for k in range(2):
                need(queue[k], *fin[b])
                t_y[k] = dma(queue[k], T.y[k::2, 128 * b:128 * b + 128], T["ysb%d" % b][k::2, 128 * k:128 * k + 128], "dy")

        for q in "vs":
            pick(q, 0)
        turn(0)
        spare(e)
        if last:
            need("v", perms["u2"])
            need("p", perms["base"])
        cast(0)
        for k in range(3):
            if k == 2:
                for q in "vs":
                    pick(q, 1)
            for q in "vs":
                look(q, 0, k)
        if last:
            place(0, 0)
            turn(1)
            place(0, 1)
            place(0, 2)
            cast(1)
        else:
            p0 = [give(0, 0)]
            turn(1)
            p0.append(give(0, 1))
            cast(1)
            evac("v", e + 1, 0, 0, p0[0])
            if e == 0:
                c_bq[1] = ranks(1, 2)
                spread(1)
                perms["l1"] = lists(1, 2)
        for k in range(len(pieces[1])):
            for q in "vs":
                look(q, 1, k)
            if k == 0 and not last:
                evac("s", e + 1, 0, 1, p0[1])
                send_codes(e + 1, 0)
            if k == 1 and last:
                for v, q in enumerate("vsvs"):
                    out(q, 0, v)
                store(0, "yy")
        need("y", ("arr%d1" % e, arrive))
        if e == 0:
            dma("y", T.tab1[0::2, :], T.tb[:, 2 * W:3 * W], "dt1")
        elif e == 1:
            t_tab[2] = dma("y", T.tab1[1::2, :], T.tb[:, 2 * W:3 * W], "dt1")
        elif e == 2:
            need("y", *zero)
            dma("y", T.tab3[0::4, 0:4096], T.tb[:, 3 * W:3 * W + W // 2], "dt3")
            t_tab[3] = dma("y", T.tab3[2::4, 4096:8192], T.tb[:, 3 * W + W // 2:4 * W], "dt3")
        if last:
            for k in range(len(pieces[1])):
                place(1, k)
            for v, q in enumerate("vsvs"):
                out(q, 1, v)
            store(1, "ys")
            need("y", *t_y.values())
            break
        p1 = [give(1, c) for c in range(2)]
        evac("v", e + 1, 1, 0, p1[0])
        evac("s", e + 1, 1, 1, p1[1])
        send_codes(e + 1, 1)
        between(e)
    need("g", *[(n, count[n]) for n in ("qv", "qs", "qp", "qg", "loc")])
